import numpy as np
import ml_dtypes


def mxq(x, axis, fmt="e4m3"):
    dtype, down = {"e4m3": (ml_dtypes.float8_e4m3fn, 7), "e5m2": (ml_dtypes.float8_e5m2, 14)}[fmt]
    v = np.moveaxis(np.asarray(x, np.float32).astype(ml_dtypes.bfloat16).astype(np.float64), axis, -1)
    blocks = v.reshape(v.shape[:-1] + (-1, 32))
    amax = np.abs(blocks).max(-1, keepdims=True)
    byte = np.maximum(np.where(amax > 0, np.frexp(amax)[1] - 1 + 127, 0) - down, 1)
    scale = np.exp2(byte - 127.0)
    codes = (blocks / scale).astype(np.float32).astype(dtype).astype(np.float64)
    return np.moveaxis((codes * scale).reshape(v.shape), -1, axis)


WIDE = False


def mx_kscale(k):
    if not WIDE:
        return np.ones(k)
    levels = np.array([10, -10, 5, -5, 0])
    if k % 512:
        return np.exp2(np.random.permutation(np.resize(levels, k // 32))).repeat(32)
    a = np.empty((k // 512, 16))
    for p in range(k // 512):
        a[p, :8] = np.random.permutation(np.resize(levels, 8))
        for g in range(8):
            far = levels[np.abs(levels - a[p, g]) >= 10]
            a[p, g + 8] = far[np.random.randint(len(far))]
    return np.exp2(a.ravel()).repeat(32)


def f64(x):
    return np.asarray(x).astype(np.float64)


def striped(idx):
    return np.tile(idx.reshape(-1, 16).T, (8, 1)).astype(np.uint16)


def unstriped(offs):
    return offs[:16].T.reshape(-1).astype(np.int64)


K, T, S, N, U = 1024, 2048, 512, 256, 1024


def setup_inputs():
    n = np.random.standard_normal
    s = mx_kscale(K)[:, None]
    return {
        "xT": (n((K, T)) * s).astype(np.float32),
        "mem": n((N, U)).astype(np.float32),
        "w1": (n((K, N)) / np.sqrt(K) / s).astype(np.float32),
        "offs": striped(np.random.permutation(T)[:S]),
        "slot": striped(np.random.permutation(U)[:S]),
    }


def reference(xT, mem, w1, offs, slot):
    xq = mxq(f64(xT)[:, unstriped(offs)], 0, "e4m3")
    y = np.tanh(mxq(f64(w1), 0, "e4m3").T @ xq)
    out = f64(mem).copy()
    out[:, unstriped(slot)] = y
    return out

@@ -1,0 +1,149 @@
+from contextlib import ExitStack
+
+import concourse.mybir as mybir
+
+K, T, S, N, U = 1024, 2048, 512, 256, 1024
+FLOPS = 2 * K * S * N
+
+F32 = mybir.dt.float32
+BF16 = mybir.dt.bfloat16
+U32 = mybir.dt.uint32
+U16 = mybir.dt.uint16
+U8 = mybir.dt.uint8
+FP8X4 = mybir.dt.float8_e4m3fn_x4
+TANH = mybir.ActivationFunctionType.Tanh
+
+P = 128
+PACK = 4
+K_PASS = P * PACK
+PASSES = K // K_PASS
+BLOCKS = N // P
+HALF = S // 2
+LIST_ROWS = 16
+
+
+def tile_picked_kvput_tanh_e_kernel(tc, xT, mem, w1, offs, slot, out):
+    nc = tc.nc
+    with ExitStack() as ctx:
+        lists = ctx.enter_context(tc.tile_pool(name="lists", bufs=1))
+        sb = ctx.enter_context(tc.tile_pool(name="sb", bufs=1))
+        psum = ctx.enter_context(tc.psum_pool(name="psum", bufs=1))
+
+        offs_sb = lists.tile([P, S // LIST_ROWS], U16, name="offs_sb")
+        slot_sb = lists.tile([P, S // LIST_ROWS], U16, name="slot_sb")
+        x_rows = xT.rearrange("(g p j) t -> g j p t", g=PASSES, j=PACK)
+        w_rows = w1.rearrange("(g p j) c -> g p j c", g=PASSES, j=PACK)
+        x_raw = [[sb.tile([P, T], F32, name="x_raw%d%d" % (g, j)) for j in range(PACK)] for g in range(PASSES)]
+        window = [sb.tile([P, U], F32, name="window%d" % b) for b in range(BLOCKS)]
+        picked = [sb.tile([P, S, PACK], BF16, align_bytes=64, name="picked%d" % g) for g in range(PASSES)]
+        acc = [[psum.tile([P, HALF], F32, name="acc%d%d" % (b, h)) for h in range(2)] for b in range(BLOCKS)]
+        w_raw = {}
+        w_mx = {}
+        x_mx = {}
+
+        warm = sb.tile([P, 1], F32, name="warm")
+        warm_out = sb.tile([P, 1], F32, name="warm_out")
+        nc.vector.memset(warm[:], 0.0)
+        nc.scalar.activation(warm_out[:], warm[:], TANH)
+
+        def load_x(g, j):
+            nc.sync.dma_start(out=x_raw[g][j][:], in_=x_rows[g, j])
+
+        def load_w(g, b0, b1):
+            raw = sb.tile([P, PACK, (b1 - b0) * P], F32, name="w_raw%d%d" % (g, b0))
+            nc.sync.dma_start(out=raw[:], in_=w_rows[g][:, :, b0 * P : b1 * P])
+            w_raw[g, b0] = raw
+
+        def load_mem(b):
+            nc.sync.dma_start(out=window[b][:], in_=mem[b * P : (b + 1) * P, :])
+
+        def quantize(src, width, tag):
+            codes = sb.tile([P, width], U32, align_bytes=64, name="codes" + tag)
+            scales = sb.tile([P, width], U8, align_bytes=64, name="scales" + tag)
+            nc.vector.quantize_mx(out=codes[:].bitcast(FP8X4), scales=scales[:], in_=src)
+            return codes, scales
+
+        def prep_w(g, b0, b1):
+            width = (b1 - b0) * P
+            grouped = sb.tile([P, width, PACK], BF16, align_bytes=64, name="w_grp%d%d" % (g, b0))
+            nc.scalar.copy(
+                out=grouped[:].rearrange("p (c i) t -> p c t i", i=4),
+                in_=w_raw[g, b0][:].rearrange("p t (c i) -> p c t i", i=4),
+            )
+            codes, scales = quantize(grouped[:].rearrange("p c t -> p (c t)"), width, "w%d%d" % (g, b0))
+            for b in range(b0, b1):
+                cols = slice((b - b0) * P, (b - b0 + 1) * P)
+                w_mx[g, b] = (codes[:, cols], scales[:, cols])
+
+        def gather(g, j, s0, s1):
+            nc.vector.tensor_copy(
+                out=picked[g][:, s0:s1, j],
+                in_=x_raw[g][j][:].indirect(offs_sb[:, s0 // LIST_ROWS : s1 // LIST_ROWS]),
+            )
+
+        def quant_x(g, h0, h1):
+            src = picked[g][:].rearrange("p s t -> p (s t)")[:, h0 * HALF * PACK : h1 * HALF * PACK]
+            codes, scales = quantize(src, (h1 - h0) * HALF, "x%d%d" % (g, h0))
+            for h in range(h0, h1):
+                cols = slice((h - h0) * HALF, (h - h0 + 1) * HALF)
+                x_mx[g, h] = (codes[:, cols], scales[:, cols])
+
+        def matmul(g, b, h):
+            nc.tensor.matmul_mx(
+                out=acc[b][h][:],
+                lhsT=w_mx[g, b][0].bitcast(FP8X4),
+                lhsT_scale=w_mx[g, b][1],
+                rhs=x_mx[g, h][0].bitcast(FP8X4),
+                rhs_scale=x_mx[g, h][1],
+                start=(g == 0),
+                stop=(g == PASSES - 1),
+            )
+
+        y = [sb.tile([P, S], F32, name="y%d" % b) for b in range(BLOCKS)]
+
+        def tanh(b, h):
+            nc.scalar.activation(y[b][:, h * HALF : (h + 1) * HALF], acc[b][h][:], TANH)
+
+        def scatter(b, s0, s1):
+            nc.vector.tensor_copy(
+                out=window[b][:].indirect(slot_sb[:, s0 // LIST_ROWS : s1 // LIST_ROWS]),
+                in_=y[b][:, s0:s1],
+            )
+
+        def store(b):
+            nc.sync.dma_start(out=out[b * P : (b + 1) * P, :], in_=window[b][:])
+
+        load_x(0, 0)
+        nc.sync.dma_start(offs_sb[:], offs)
+        for j in range(1, PACK):
+            load_x(0, j)
+        load_w(0, 0, 2)
+        load_w(1, 0, 2)
+        for j in range(PACK):
+            load_x(1, j)
+        nc.sync.dma_start(slot_sb[:], slot)
+        load_mem(0)
+        load_mem(1)
+        for j in range(PACK):
+            gather(0, j, 0, S)
+        quant_x(0, 0, 2)
+        prep_w(0, 0, 2)
+        prep_w(1, 0, 2)
+        for b in range(BLOCKS):
+            for h in range(2):
+                matmul(0, b, h)
+        for j in range(PACK - 1):
+            gather(1, j, 0, S)
+        for h in range(2):
+            gather(1, PACK - 1, h * HALF, (h + 1) * HALF)
+            quant_x(1, h, h + 1)
+            for b in range(BLOCKS):
+                matmul(1, b, h)
+        for b in range(BLOCKS):
+            for h in range(2):
+                tanh(b, h)
+        scatter(0, 0, HALF)
+        scatter(0, HALF, S)
+        store(0)
+        scatter(1, 0, S)
+        store(1)

@@ -19,6 +19,7 @@ K_PASS = P * PACK
 PASSES = K // K_PASS
 BLOCKS = N // P
 HALF = S // 2
+QUARTER = S // 4
 LIST_ROWS = 16
 
 
@@ -33,13 +34,9 @@ def tile_picked_kvput_tanh_e_kernel(tc, xT, mem, w1, offs, slot, out):
         slot_sb = lists.tile([P, S // LIST_ROWS], U16, name="slot_sb")
         x_rows = xT.rearrange("(g p j) t -> g j p t", g=PASSES, j=PACK)
         w_rows = w1.rearrange("(g p j) c -> g p j c", g=PASSES, j=PACK)
-        x_raw = [[sb.tile([P, T], F32, name="x_raw%d%d" % (g, j)) for j in range(PACK)] for g in range(PASSES)]
-        window = [sb.tile([P, U], F32, name="window%d" % b) for b in range(BLOCKS)]
-        picked = [sb.tile([P, S, PACK], BF16, align_bytes=64, name="picked%d" % g) for g in range(PASSES)]
-        acc = [[psum.tile([P, HALF], F32, name="acc%d%d" % (b, h)) for h in range(2)] for b in range(BLOCKS)]
+        x_raw = {}
         w_raw = {}
-        w_mx = {}
-        x_mx = {}
+        window = {}
 
         warm = sb.tile([P, 1], F32, name="warm")
         warm_out = sb.tile([P, 1], F32, name="warm_out")
@@ -47,103 +44,108 @@ def tile_picked_kvput_tanh_e_kernel(tc, xT, mem, w1, offs, slot, out):
         nc.scalar.activation(warm_out[:], warm[:], TANH)
 
         def load_x(g, j):
-            nc.sync.dma_start(out=x_raw[g][j][:], in_=x_rows[g, j])
+            x_raw[g, j] = sb.tile([P, T], F32, name="x_raw%d%d" % (g, j))
+            nc.sync.dma_start(out=x_raw[g, j][:], in_=x_rows[g, j])
 
-        def load_w(g, b0, b1):
-            raw = sb.tile([P, PACK, (b1 - b0) * P], F32, name="w_raw%d%d" % (g, b0))
-            nc.sync.dma_start(out=raw[:], in_=w_rows[g][:, :, b0 * P : b1 * P])
-            w_raw[g, b0] = raw
+        def load_w(g, b):
+            w_raw[g, b] = sb.tile([P, PACK, P], F32, align_bytes=64, name="w_raw%d%d" % (g, b))
+            nc.sync.dma_start(out=w_raw[g, b][:], in_=w_rows[g][:, :, b * P : (b + 1) * P])
 
         def load_mem(b):
+            window[b] = sb.tile([P, U], F32, name="window%d" % b)
             nc.sync.dma_start(out=window[b][:], in_=mem[b * P : (b + 1) * P, :])
 
-        def quantize(src, width, tag):
-            codes = sb.tile([P, width], U32, align_bytes=64, name="codes" + tag)
-            scales = sb.tile([P, width], U8, align_bytes=64, name="scales" + tag)
+        def quantize(src, name, codes_tag):
+            width = src.shape[1] // PACK
+            codes = sb.tile([P, width], U32, align_bytes=64, name="codes_" + name, tag=codes_tag)
+            scales = sb.tile([P, width], U8, align_bytes=64, name="scales_" + name)
             nc.vector.quantize_mx(out=codes[:].bitcast(FP8X4), scales=scales[:], in_=src)
             return codes, scales
 
-        def prep_w(g, b0, b1):
-            width = (b1 - b0) * P
-            grouped = sb.tile([P, width, PACK], BF16, align_bytes=64, name="w_grp%d%d" % (g, b0))
+        def quantize_w(g, b):
+            grouped = sb.tile([P, P, PACK], BF16, align_bytes=64, name="w_grouped%d%d" % (g, b))
             nc.scalar.copy(
                 out=grouped[:].rearrange("p (c i) t -> p c t i", i=4),
-                in_=w_raw[g, b0][:].rearrange("p t (c i) -> p c t i", i=4),
+                in_=w_raw[g, b][:].rearrange("p t (c i) -> p c t i", i=4),
             )
-            codes, scales = quantize(grouped[:].rearrange("p c t -> p (c t)"), width, "w%d%d" % (g, b0))
-            for b in range(b0, b1):
-                cols = slice((b - b0) * P, (b - b0 + 1) * P)
-                w_mx[g, b] = (codes[:, cols], scales[:, cols])
+            name = "w%d%d" % (g, b)
+            return quantize(grouped[:].rearrange("p c t -> p (c t)"), name, "codes_" + name)
 
-        def gather(g, j, s0, s1):
-            nc.vector.tensor_copy(
-                out=picked[g][:, s0:s1, j],
-                in_=x_raw[g][j][:].indirect(offs_sb[:, s0 // LIST_ROWS : s1 // LIST_ROWS]),
-            )
+        def entries(list_sb, s0, s1):
+            return list_sb[:, s0 // LIST_ROWS : s1 // LIST_ROWS]
 
-        def quant_x(g, h0, h1):
-            src = picked[g][:].rearrange("p s t -> p (s t)")[:, h0 * HALF * PACK : h1 * HALF * PACK]
-            codes, scales = quantize(src, (h1 - h0) * HALF, "x%d%d" % (g, h0))
-            for h in range(h0, h1):
-                cols = slice((h - h0) * HALF, (h - h0 + 1) * HALF)
-                x_mx[g, h] = (codes[:, cols], scales[:, cols])
+        def gather_pass(g):
+            picked = sb.tile([P, S, PACK], BF16, align_bytes=64, name="picked%d" % g)
+            for j in range(PACK):
+                nc.vector.tensor_copy(out=picked[:, :, j], in_=x_raw[g, j][:].indirect(offs_sb[:]))
+            return picked[:].rearrange("p s t -> p (s t)")
 
-        def matmul(g, b, h):
+        def matmul(acc, w_mx, x_mx, cols, g):
             nc.tensor.matmul_mx(
-                out=acc[b][h][:],
-                lhsT=w_mx[g, b][0].bitcast(FP8X4),
-                lhsT_scale=w_mx[g, b][1],
-                rhs=x_mx[g, h][0].bitcast(FP8X4),
-                rhs_scale=x_mx[g, h][1],
+                out=acc[:],
+                lhsT=w_mx[0][:].bitcast(FP8X4),
+                lhsT_scale=w_mx[1][:],
+                rhs=x_mx[0][:, cols].bitcast(FP8X4),
+                rhs_scale=x_mx[1][:, cols],
                 start=(g == 0),
                 stop=(g == PASSES - 1),
             )
 
-        y = [sb.tile([P, S], F32, name="y%d" % b) for b in range(BLOCKS)]
-
-        def tanh(b, h):
-            nc.scalar.activation(y[b][:, h * HALF : (h + 1) * HALF], acc[b][h][:], TANH)
-
-        def scatter(b, s0, s1):
-            nc.vector.tensor_copy(
-                out=window[b][:].indirect(slot_sb[:, s0 // LIST_ROWS : s1 // LIST_ROWS]),
-                in_=y[b][:, s0:s1],
-            )
+        def finish(b, s0, s1, acc, y_tag):
+            y = sb.tile([P, s1 - s0], F32, align_bytes=64, name="y%d_%d" % (b, s0), tag=y_tag)
+            nc.scalar.activation(y[:], acc[:], TANH)
+            nc.vector.tensor_copy(out=window[b][:].indirect(entries(slot_sb, s0, s1)), in_=y[:])
 
         def store(b):
             nc.sync.dma_start(out=out[b * P : (b + 1) * P, :], in_=window[b][:])
 
         load_x(0, 0)
         nc.sync.dma_start(offs_sb[:], offs)
-        for j in range(1, PACK):
-            load_x(0, j)
-        load_w(0, 0, 2)
-        load_w(1, 0, 2)
-        for j in range(PACK):
-            load_x(1, j)
         nc.sync.dma_start(slot_sb[:], slot)
+        for g in range(PASSES):
+            for j in range(PACK):
+                if (g, j) != (0, 0):
+                    load_x(g, j)
+        load_w(0, 0)
+        load_w(1, 0)
         load_mem(0)
+        load_w(0, 1)
+        load_w(1, 1)
         load_mem(1)
-        for j in range(PACK):
-            gather(0, j, 0, S)
-        quant_x(0, 0, 2)
-        prep_w(0, 0, 2)
-        prep_w(1, 0, 2)
+
+        pieces = {0: [(0, QUARTER), (QUARTER, HALF), (HALF, S)], 1: [(0, HALF), (HALF, S)]}
+        acc = {}
         for b in range(BLOCKS):
-            for h in range(2):
-                matmul(0, b, h)
-        for j in range(PACK - 1):
-            gather(1, j, 0, S)
-        for h in range(2):
-            gather(1, PACK - 1, h * HALF, (h + 1) * HALF)
-            quant_x(1, h, h + 1)
-            for b in range(BLOCKS):
-                matmul(1, b, h)
-        for b in range(BLOCKS):
-            for h in range(2):
-                tanh(b, h)
-        scatter(0, 0, HALF)
-        scatter(0, HALF, S)
+            for s0, s1 in pieces[b]:
+                acc[b, s0] = psum.tile([P, s1 - s0], F32, name="acc%d_%d" % (b, s0))
+
+        x0_mx = quantize(gather_pass(0), "x0", "codes_x0")
+        picked1 = gather_pass(1)
+        x1_mx = {}
+
+        def pass0(b):
+            w_mx = quantize_w(0, b)
+            for s0, s1 in pieces[b]:
+                matmul(acc[b, s0], w_mx, x0_mx, slice(s0, s1), 0)
+
+        def pass1(b, w_mx, s0, s1):
+            h = s0 // HALF
+            matmul(acc[b, s0], w_mx, x1_mx[h], slice(s0 - h * HALF, s1 - h * HALF), 1)
+
+        pass0(0)
+        x1_mx[0] = quantize(picked1[:, 0 : HALF * PACK], "x10", "w_grouped00")
+        w10_mx = quantize_w(1, 0)
+        x1_mx[1] = quantize(picked1[:, HALF * PACK : S * PACK], "x11", "w_grouped10")
+        for s0, s1 in pieces[0]:
+            pass1(0, w10_mx, s0, s1)
+        for s0, s1 in pieces[0][:2]:
+            finish(0, s0, s1, acc[0, s0], "y0_%d" % s0)
+        pass0(1)
+        w11_mx = quantize_w(1, 1)
+        for s0, s1 in pieces[1]:
+            pass1(1, w11_mx, s0, s1)
+        finish(0, HALF, S, acc[0, HALF], "w_raw11")
         store(0)
-        scatter(1, 0, S)
+        for s0, s1 in pieces[1]:
+            finish(1, s0, s1, acc[1, s0], "y1_%d" % s0)
         store(1)

@@ -62,8 +62,8 @@ def tile_picked_kvput_tanh_e_kernel(tc, xT, mem, w1, offs, slot, out):
             nc.vector.quantize_mx(out=codes[:].bitcast(FP8X4), scales=scales[:], in_=src)
             return codes, scales
 
-        def quantize_w(g, b):
-            grouped = sb.tile([P, P, PACK], BF16, align_bytes=64, name="w_grouped%d%d" % (g, b))
+        def quantize_w(g, b, tag):
+            grouped = sb.tile([P, P, PACK], BF16, align_bytes=64, name="w_grouped%d%d" % (g, b), tag=tag)
             nc.scalar.copy(
                 out=grouped[:].rearrange("p (c i) t -> p c t i", i=4),
                 in_=w_raw[g, b][:].rearrange("p t (c i) -> p c t i", i=4),
@@ -91,9 +91,10 @@ def tile_picked_kvput_tanh_e_kernel(tc, xT, mem, w1, offs, slot, out):
                 stop=(g == PASSES - 1),
             )
 
-        def finish(b, s0, s1, acc, y_tag):
-            y = sb.tile([P, s1 - s0], F32, align_bytes=64, name="y%d_%d" % (b, s0), tag=y_tag)
-            nc.scalar.activation(y[:], acc[:], TANH)
+        def tanh(y, acc):
+            nc.scalar.activation(y, acc[:], TANH)
+
+        def scatter(b, s0, s1, y):
             nc.vector.tensor_copy(out=window[b][:].indirect(entries(slot_sb, s0, s1)), in_=y[:])
 
         def store(b):
@@ -113,39 +114,35 @@ def tile_picked_kvput_tanh_e_kernel(tc, xT, mem, w1, offs, slot, out):
         load_w(1, 1)
         load_mem(1)
 
-        pieces = {0: [(0, QUARTER), (QUARTER, HALF), (HALF, S)], 1: [(0, HALF), (HALF, S)]}
-        acc = {}
-        for b in range(BLOCKS):
-            for s0, s1 in pieces[b]:
-                acc[b, s0] = psum.tile([P, s1 - s0], F32, name="acc%d_%d" % (b, s0))
-
+        acc = [[psum.tile([P, HALF], F32, name="acc%d%d" % (b, h)) for h in range(2)] for b in range(BLOCKS)]
         x0_mx = quantize(gather_pass(0), "x0", "codes_x0")
         picked1 = gather_pass(1)
         x1_mx = {}
 
-        def pass0(b):
-            w_mx = quantize_w(0, b)
-            for s0, s1 in pieces[b]:
-                matmul(acc[b, s0], w_mx, x0_mx, slice(s0, s1), 0)
+        def pass0(b, w_mx):
+            for h in range(2):
+                matmul(acc[b][h], w_mx, x0_mx, slice(h * HALF, (h + 1) * HALF), 0)
 
-        def pass1(b, w_mx, s0, s1):
-            h = s0 // HALF
-            matmul(acc[b, s0], w_mx, x1_mx[h], slice(s0 - h * HALF, s1 - h * HALF), 1)
+        def pass1(b, w_mx):
+            for h in range(2):
+                matmul(acc[b][h], w_mx, x1_mx[h], slice(0, HALF), 1)
 
-        pass0(0)
+        pass0(0, quantize_w(0, 0, "w_grouped00"))
         x1_mx[0] = quantize(picked1[:, 0 : HALF * PACK], "x10", "w_grouped00")
-        w10_mx = quantize_w(1, 0)
+        w10_mx = quantize_w(1, 0, "w_grouped10")
         x1_mx[1] = quantize(picked1[:, HALF * PACK : S * PACK], "x11", "w_grouped10")
-        for s0, s1 in pieces[0]:
-            pass1(0, w10_mx, s0, s1)
-        for s0, s1 in pieces[0][:2]:
-            finish(0, s0, s1, acc[0, s0], "y0_%d" % s0)
-        pass0(1)
-        w11_mx = quantize_w(1, 1)
-        for s0, s1 in pieces[1]:
-            pass1(1, w11_mx, s0, s1)
-        finish(0, HALF, S, acc[0, HALF], "w_raw11")
+        pass1(0, w10_mx)
+        y00 = sb.tile([P, HALF], F32, name="y00")
+        tanh(y00[:], acc[0][0])
+        scatter(0, 0, HALF, y00)
+        pass0(1, quantize_w(0, 1, "codes_w10"))
+        pass1(1, quantize_w(1, 1, "w_grouped11"))
+        y01 = sb.tile([P, HALF], F32, align_bytes=64, name="y01", tag="w_raw11")
+        tanh(y01[:], acc[0][1])
+        scatter(0, HALF, S, y01)
         store(0)
-        for s0, s1 in pieces[1]:
-            finish(1, s0, s1, acc[1, s0], "y1_%d" % s0)
+        y1 = sb.tile([P, S], F32, name="y1")
+        for h in range(2):
+            tanh(y1[:, h * HALF : (h + 1) * HALF], acc[1][h])
+        scatter(1, 0, S, y1)
         store(1)

@@ -12,6 +12,7 @@ U16 = mybir.dt.uint16
 U8 = mybir.dt.uint8
 FP8X4 = mybir.dt.float8_e4m3fn_x4
 TANH = mybir.ActivationFunctionType.Tanh
+COPY = mybir.ActivationFunctionType.Copy
 
 P = 128
 PACK = 4
@@ -47,102 +48,92 @@ def tile_picked_kvput_tanh_e_kernel(tc, xT, mem, w1, offs, slot, out):
             x_raw[g, j] = sb.tile([P, T], F32, name="x_raw%d%d" % (g, j))
             nc.sync.dma_start(out=x_raw[g, j][:], in_=x_rows[g, j])
 
-        def load_w(g, b):
-            w_raw[g, b] = sb.tile([P, PACK, P], F32, align_bytes=64, name="w_raw%d%d" % (g, b))
-            nc.sync.dma_start(out=w_raw[g, b][:], in_=w_rows[g][:, :, b * P : (b + 1) * P])
+        def load_w(g):
+            w_raw[g] = sb.tile([P, PACK, N], F32, align_bytes=64, name="w_raw%d" % g)
+            nc.sync.dma_start(out=w_raw[g][:], in_=w_rows[g])
 
         def load_mem(b):
             window[b] = sb.tile([P, U], F32, name="window%d" % b)
             nc.sync.dma_start(out=window[b][:], in_=mem[b * P : (b + 1) * P, :])
 
-        def quantize(src, name, codes_tag):
+        def quantize(src, name):
             width = src.shape[1] // PACK
-            codes = sb.tile([P, width], U32, align_bytes=64, name="codes_" + name, tag=codes_tag)
+            codes = sb.tile([P, width], U32, align_bytes=64, name="codes_" + name)
             scales = sb.tile([P, width], U8, align_bytes=64, name="scales_" + name)
             nc.vector.quantize_mx(out=codes[:].bitcast(FP8X4), scales=scales[:], in_=src)
             return codes, scales
 
-        def quantize_w(g, b, tag):
-            grouped = sb.tile([P, P, PACK], BF16, align_bytes=64, name="w_grouped%d%d" % (g, b), tag=tag)
+        def quantize_w(g):
+            grouped = sb.tile([P, N, PACK], BF16, align_bytes=64, name="w_grouped%d" % g)
             nc.scalar.copy(
                 out=grouped[:].rearrange("p (c i) t -> p c t i", i=4),
-                in_=w_raw[g, b][:].rearrange("p t (c i) -> p c t i", i=4),
+                in_=w_raw[g][:].rearrange("p t (c i) -> p c t i", i=4),
             )
-            name = "w%d%d" % (g, b)
-            return quantize(grouped[:].rearrange("p c t -> p (c t)"), name, "codes_" + name)
+            return quantize(grouped[:].rearrange("p c t -> p (c t)"), "w%d" % g)
 
         def entries(list_sb, s0, s1):
             return list_sb[:, s0 // LIST_ROWS : s1 // LIST_ROWS]
 
-        def gather_pass(g):
-            picked = sb.tile([P, S, PACK], BF16, align_bytes=64, name="picked%d" % g)
-            for j in range(PACK):
-                nc.vector.tensor_copy(out=picked[:, :, j], in_=x_raw[g, j][:].indirect(offs_sb[:]))
-            return picked[:].rearrange("p s t -> p (s t)")
+        def gather(picked, g, j, s0, s1):
+            nc.vector.tensor_copy(out=picked[:, s0:s1, j], in_=x_raw[g, j][:].indirect(entries(offs_sb, s0, s1)))
 
-        def matmul(acc, w_mx, x_mx, cols, g):
+        def matmul(acc, w_mx, b, x_mx, cols, g):
             nc.tensor.matmul_mx(
                 out=acc[:],
-                lhsT=w_mx[0][:].bitcast(FP8X4),
-                lhsT_scale=w_mx[1][:],
+                lhsT=w_mx[0][:, b * P : (b + 1) * P].bitcast(FP8X4),
+                lhsT_scale=w_mx[1][:, b * P : (b + 1) * P],
                 rhs=x_mx[0][:, cols].bitcast(FP8X4),
                 rhs_scale=x_mx[1][:, cols],
                 start=(g == 0),
                 stop=(g == PASSES - 1),
             )
 
-        def tanh(y, acc):
-            nc.scalar.activation(y, acc[:], TANH)
+        def tanh(b, h):
+            nc.scalar.activation(y[b][:, h * HALF : (h + 1) * HALF], acc[b][h][:], TANH)
 
-        def scatter(b, s0, s1, y):
-            nc.vector.tensor_copy(out=window[b][:].indirect(entries(slot_sb, s0, s1)), in_=y[:])
+        def scatter_vector(b, s0, s1):
+            nc.vector.tensor_copy(out=window[b][:].indirect(entries(slot_sb, s0, s1)), in_=y[b][:, s0:s1])
 
-        def store(b):
-            nc.sync.dma_start(out=out[b * P : (b + 1) * P, :], in_=window[b][:])
+        def scatter_scalar(b, s0, s1):
+            nc.scalar.activation(window[b][:].indirect(entries(slot_sb, s0, s1)), y[b][:, s0:s1], COPY)
 
         load_x(0, 0)
         nc.sync.dma_start(offs_sb[:], offs)
         nc.sync.dma_start(slot_sb[:], slot)
+        load_x(0, 1)
+        load_w(0)
+        load_w(1)
         for g in range(PASSES):
             for j in range(PACK):
-                if (g, j) != (0, 0):
+                if (g, j) not in x_raw:
                     load_x(g, j)
-        load_w(0, 0)
-        load_w(1, 0)
-        load_mem(0)
-        load_w(0, 1)
-        load_w(1, 1)
         load_mem(1)
+        load_mem(0)
 
         acc = [[psum.tile([P, HALF], F32, name="acc%d%d" % (b, h)) for h in range(2)] for b in range(BLOCKS)]
-        x0_mx = quantize(gather_pass(0), "x0", "codes_x0")
-        picked1 = gather_pass(1)
-        x1_mx = {}
-
-        def pass0(b, w_mx):
+        picked = [sb.tile([P, S, PACK], BF16, align_bytes=64, name="picked%d" % g) for g in range(PASSES)]
+        w_mx = [quantize_w(g) for g in range(PASSES)]
+        for j in range(PACK):
+            gather(picked[0], 0, j, 0, S)
+        x0_mx = quantize(picked[0][:].rearrange("p s t -> p (s t)"), "x0")
+        for b in range(BLOCKS):
             for h in range(2):
-                matmul(acc[b][h], w_mx, x0_mx, slice(h * HALF, (h + 1) * HALF), 0)
-
-        def pass1(b, w_mx):
-            for h in range(2):
-                matmul(acc[b][h], w_mx, x1_mx[h], slice(0, HALF), 1)
-
-        pass0(0, quantize_w(0, 0, "w_grouped00"))
-        x1_mx[0] = quantize(picked1[:, 0 : HALF * PACK], "x10", "w_grouped00")
-        w10_mx = quantize_w(1, 0, "w_grouped10")
-        x1_mx[1] = quantize(picked1[:, HALF * PACK : S * PACK], "x11", "w_grouped10")
-        pass1(0, w10_mx)
-        y00 = sb.tile([P, HALF], F32, name="y00")
-        tanh(y00[:], acc[0][0])
-        scatter(0, 0, HALF, y00)
-        pass0(1, quantize_w(0, 1, "codes_w10"))
-        pass1(1, quantize_w(1, 1, "w_grouped11"))
-        y01 = sb.tile([P, HALF], F32, align_bytes=64, name="y01", tag="w_raw11")
-        tanh(y01[:], acc[0][1])
-        scatter(0, HALF, S, y01)
-        store(0)
-        y1 = sb.tile([P, S], F32, name="y1")
+                matmul(acc[b][h], w_mx[0], b, x0_mx, slice(h * HALF, (h + 1) * HALF), 0)
+        for j in range(PACK - 1):
+            gather(picked[1], 1, j, 0, S)
         for h in range(2):
-            tanh(y1[:, h * HALF : (h + 1) * HALF], acc[1][h])
-        scatter(1, 0, S, y1)
-        store(1)
+            gather(picked[1], 1, PACK - 1, h * HALF, (h + 1) * HALF)
+            x1_mx = quantize(picked[1][:, h * HALF : (h + 1) * HALF, :].rearrange("p s t -> p (s t)"), "x1%d" % h)
+            for b in (1, 0):
+                matmul(acc[b][h], w_mx[1], b, x1_mx, slice(0, HALF), 1)
+        y = [sb.tile([P, S], F32, name="y%d" % b) for b in range(BLOCKS)]
+        tanh(1, 0)
+        scatter_vector(1, 0, HALF)
+        tanh(0, 0)
+        scatter_scalar(0, 0, QUARTER)
+        tanh(1, 1)
+        scatter_vector(1, HALF, S)
+        tanh(0, 1)
+        scatter_scalar(0, QUARTER, S)
+        for b in (1, 0):
+            nc.sync.dma_start(out=out[b * P : (b + 1) * P, :], in_=window[b][:])

@@ -48,9 +48,11 @@ def tile_picked_kvput_tanh_e_kernel(tc, xT, mem, w1, offs, slot, out):
             x_raw[g, j] = sb.tile([P, T], F32, name="x_raw%d%d" % (g, j))
             nc.sync.dma_start(out=x_raw[g, j][:], in_=x_rows[g, j])
 
-        def load_w(g):
-            w_raw[g] = sb.tile([P, PACK, N], F32, align_bytes=64, name="w_raw%d" % g)
-            nc.sync.dma_start(out=w_raw[g][:], in_=w_rows[g])
+        def load_w(g, b0, b1):
+            raw = sb.tile([P, PACK, (b1 - b0) * P], F32, align_bytes=64, name="w_raw%d%d" % (g, b0))
+            nc.sync.dma_start(out=raw[:], in_=w_rows[g][:, :, b0 * P : b1 * P])
+            for b in range(b0, b1):
+                w_raw[g, b] = raw[:, :, (b - b0) * P : (b - b0 + 1) * P]
 
         def load_mem(b):
             window[b] = sb.tile([P, U], F32, name="window%d" % b)
@@ -63,13 +65,13 @@ def tile_picked_kvput_tanh_e_kernel(tc, xT, mem, w1, offs, slot, out):
             nc.vector.quantize_mx(out=codes[:].bitcast(FP8X4), scales=scales[:], in_=src)
             return codes, scales
 
-        def quantize_w(g):
-            grouped = sb.tile([P, N, PACK], BF16, align_bytes=64, name="w_grouped%d" % g)
+        def quantize_w(g, b):
+            grouped = sb.tile([P, P, PACK], BF16, align_bytes=64, name="w_grouped%d%d" % (g, b))
             nc.scalar.copy(
                 out=grouped[:].rearrange("p (c i) t -> p c t i", i=4),
-                in_=w_raw[g][:].rearrange("p t (c i) -> p c t i", i=4),
+                in_=w_raw[g, b].rearrange("p t (c i) -> p c t i", i=4),
             )
-            return quantize(grouped[:].rearrange("p c t -> p (c t)"), "w%d" % g)
+            return quantize(grouped[:].rearrange("p c t -> p (c t)"), "w%d%d" % (g, b))
 
         def entries(list_sb, s0, s1):
             return list_sb[:, s0 // LIST_ROWS : s1 // LIST_ROWS]
@@ -77,19 +79,26 @@ def tile_picked_kvput_tanh_e_kernel(tc, xT, mem, w1, offs, slot, out):
         def gather(picked, g, j, s0, s1):
             nc.vector.tensor_copy(out=picked[:, s0:s1, j], in_=x_raw[g, j][:].indirect(entries(offs_sb, s0, s1)))
 
-        def matmul(acc, w_mx, b, x_mx, cols, g):
+        def matmul(g, b, s0, s1):
             nc.tensor.matmul_mx(
-                out=acc[:],
-                lhsT=w_mx[0][:, b * P : (b + 1) * P].bitcast(FP8X4),
-                lhsT_scale=w_mx[1][:, b * P : (b + 1) * P],
-                rhs=x_mx[0][:, cols].bitcast(FP8X4),
-                rhs_scale=x_mx[1][:, cols],
+                out=acc[b, s0][:],
+                lhsT=w_mx[g, b][0][:].bitcast(FP8X4),
+                lhsT_scale=w_mx[g, b][1][:],
+                rhs=x_codes[g, s0 // HALF][:, s0 % HALF : s0 % HALF + s1 - s0].bitcast(FP8X4),
+                rhs_scale=x_scales[g][:, s0:s1],
                 start=(g == 0),
                 stop=(g == PASSES - 1),
             )
 
-        def tanh(b, h):
-            nc.scalar.activation(y[b][:, h * HALF : (h + 1) * HALF], acc[b][h][:], TANH)
+        def quantize_x(g, s0, s1):
+            nc.vector.quantize_mx(
+                out=x_codes[g, s0 // HALF][:, s0 % HALF : s0 % HALF + s1 - s0].bitcast(FP8X4),
+                scales=x_scales[g][:, s0:s1],
+                in_=picked[g][:, s0:s1, :].rearrange("p s t -> p (s t)"),
+            )
+
+        def tanh(b, s0, s1):
+            nc.scalar.activation(y[b][:, s0:s1], acc[b, s0][:], TANH)
 
         def scatter_vector(b, s0, s1):
             nc.vector.tensor_copy(out=window[b][:].indirect(entries(slot_sb, s0, s1)), in_=y[b][:, s0:s1])
@@ -99,41 +108,56 @@ def tile_picked_kvput_tanh_e_kernel(tc, xT, mem, w1, offs, slot, out):
 
         load_x(0, 0)
         nc.sync.dma_start(offs_sb[:], offs)
-        nc.sync.dma_start(slot_sb[:], slot)
         load_x(0, 1)
-        load_w(0)
-        load_w(1)
+        load_w(0, 0, 2)
+        load_w(1, 1, 2)
         for g in range(PASSES):
             for j in range(PACK):
                 if (g, j) not in x_raw:
                     load_x(g, j)
+        load_w(1, 0, 1)
+        nc.sync.dma_start(slot_sb[:], slot)
         load_mem(1)
         load_mem(0)
 
-        acc = [[psum.tile([P, HALF], F32, name="acc%d%d" % (b, h)) for h in range(2)] for b in range(BLOCKS)]
+        pieces = [(1, 0, QUARTER), (1, QUARTER, HALF), (0, 0, HALF), (1, HALF, S), (0, HALF, S)]
+        acc = {(b, s0): psum.tile([P, s1 - s0], F32, name="acc%d_%d" % (b, s0)) for b, s0, s1 in pieces}
         picked = [sb.tile([P, S, PACK], BF16, align_bytes=64, name="picked%d" % g) for g in range(PASSES)]
-        w_mx = [quantize_w(g) for g in range(PASSES)]
+        x_codes = {
+            (g, h): sb.tile([P, HALF], U32, align_bytes=64, name="x_codes%d%d" % (g, h))
+            for g, h in ((0, 0), (0, 1), (1, 0))
+        }
+        x_scales = [sb.tile([P, S], U8, align_bytes=64, name="x_scales%d" % g) for g in range(PASSES)]
+        y = [sb.tile([P, S], F32, name="y%d" % b) for b in range(BLOCKS)]
+        w_mx = {(g, b): quantize_w(g, b) for g, b in ((0, 0), (0, 1), (1, 1))}
         for j in range(PACK):
             gather(picked[0], 0, j, 0, S)
-        x0_mx = quantize(picked[0][:].rearrange("p s t -> p (s t)"), "x0")
-        for b in range(BLOCKS):
-            for h in range(2):
-                matmul(acc[b][h], w_mx[0], b, x0_mx, slice(h * HALF, (h + 1) * HALF), 0)
-        for j in range(PACK - 1):
+        quantize_x(0, 0, HALF)
+        quantize_x(0, HALF, S)
+        for b, s0, s1 in pieces:
+            matmul(0, b, s0, s1)
+        last = PACK - 1
+        for j in range(last):
             gather(picked[1], 1, j, 0, S)
-        for h in range(2):
-            gather(picked[1], 1, PACK - 1, h * HALF, (h + 1) * HALF)
-            x1_mx = quantize(picked[1][:, h * HALF : (h + 1) * HALF, :].rearrange("p s t -> p (s t)"), "x1%d" % h)
-            for b in (1, 0):
-                matmul(acc[b][h], w_mx[1], b, x1_mx, slice(0, HALF), 1)
-        y = [sb.tile([P, S], F32, name="y%d" % b) for b in range(BLOCKS)]
-        tanh(1, 0)
-        scatter_vector(1, 0, HALF)
-        tanh(0, 0)
-        scatter_scalar(0, 0, QUARTER)
-        tanh(1, 1)
-        scatter_vector(1, HALF, S)
-        tanh(0, 1)
-        scatter_scalar(0, QUARTER, S)
+        plain = sb.tile([P, HALF], BF16, name="plain")
+        gather(picked[1], 1, last, 0, HALF)
+        nc.scalar.activation(plain[:], x_raw[1, last][:].indirect(entries(offs_sb, HALF, S)), COPY)
+        nc.vector.tensor_copy(out=picked[1][:, HALF:S, last], in_=plain[:])
+        for b, s0, s1 in pieces[:2]:
+            quantize_x(1, s0, s1)
+        w_mx[1, 0] = quantize_w(1, 0)
+        x_codes[1, 1] = sb.tile([P, HALF], U32, align_bytes=64, name="x_codes11", tag="w_raw10")
+        quantize_x(1, HALF, S)
+        for b, s0, s1 in pieces:
+            matmul(1, b, s0, s1)
+        tanh(1, 0, QUARTER)
+        scatter_vector(1, 0, QUARTER)
+        tanh(1, QUARTER, HALF)
+        tanh(0, 0, HALF)
+        tanh(1, HALF, S)
+        scatter_vector(1, QUARTER, S)
+        scatter_scalar(0, 0, HALF)
+        tanh(0, HALF, S)
+        scatter_scalar(0, HALF, S)
         for b in (1, 0):
             nc.sync.dma_start(out=out[b * P : (b + 1) * P, :], in_=window[b][:])

@@ -33,10 +33,9 @@ def tile_picked_kvput_tanh_e_kernel(tc, xT, mem, w1, offs, slot, out):
 
         offs_sb = lists.tile([P, S // LIST_ROWS], U16, name="offs_sb")
         slot_sb = lists.tile([P, S // LIST_ROWS], U16, name="slot_sb")
-        x_rows = xT.rearrange("(g p j) t -> g j p t", g=PASSES, j=PACK)
-        w_rows = w1.rearrange("(g p j) c -> g p j c", g=PASSES, j=PACK)
+        x_rows = xT.rearrange("(g p j) t -> g p j t", g=PASSES, j=PACK)
+        w_rows = w1.rearrange("(g p j) c -> p g (j c)", g=PASSES, j=PACK)
         x_raw = {}
-        w_raw = {}
         window = {}
 
         warm = sb.tile([P, 1], F32, name="warm")
@@ -44,47 +43,40 @@ def tile_picked_kvput_tanh_e_kernel(tc, xT, mem, w1, offs, slot, out):
         nc.vector.memset(warm[:], 0.0)
         nc.scalar.activation(warm_out[:], warm[:], TANH)
 
-        def load_x(g, j):
-            x_raw[g, j] = sb.tile([P, T], F32, name="x_raw%d%d" % (g, j))
-            nc.sync.dma_start(out=x_raw[g, j][:], in_=x_rows[g, j])
-
-        def load_w(g, b0, b1):
-            raw = sb.tile([P, PACK, (b1 - b0) * P], F32, align_bytes=64, name="w_raw%d%d" % (g, b0))
-            nc.sync.dma_start(out=raw[:], in_=w_rows[g][:, :, b0 * P : b1 * P])
-            for b in range(b0, b1):
-                w_raw[g, b] = raw[:, :, (b - b0) * P : (b - b0 + 1) * P]
+        def load_x(g, j0, j1):
+            raw = sb.tile([P, j1 - j0, T], F32, name="x_raw%d%d" % (g, j0))
+            nc.sync.dma_start(out=raw[:], in_=x_rows[g][:, j0:j1, :])
+            for j in range(j0, j1):
+                x_raw[g, j] = raw[:, j - j0, :]
 
         def load_mem(b):
             window[b] = sb.tile([P, U], F32, name="window%d" % b)
             nc.sync.dma_start(out=window[b][:], in_=mem[b * P : (b + 1) * P, :])
 
-        def quantize(src, name):
-            width = src.shape[1] // PACK
-            codes = sb.tile([P, width], U32, align_bytes=64, name="codes_" + name)
-            scales = sb.tile([P, width], U8, align_bytes=64, name="scales_" + name)
-            nc.vector.quantize_mx(out=codes[:].bitcast(FP8X4), scales=scales[:], in_=src)
-            return codes, scales
-
-        def quantize_w(g, b):
-            grouped = sb.tile([P, P, PACK], BF16, align_bytes=64, name="w_grouped%d%d" % (g, b))
+        def quantize_w(g):
+            grouped = sb.tile([P, N, PACK], BF16, align_bytes=64, name="w_grouped%d" % g)
             nc.scalar.copy(
                 out=grouped[:].rearrange("p (c i) t -> p c t i", i=4),
-                in_=w_raw[g, b].rearrange("p t (c i) -> p c t i", i=4),
+                in_=w_raw[:, g, :].rearrange("p (t c i) -> p c t i", t=PACK, i=4),
             )
-            return quantize(grouped[:].rearrange("p c t -> p (c t)"), "w%d%d" % (g, b))
+            nc.vector.quantize_mx(
+                out=w_codes[g][:].bitcast(FP8X4),
+                scales=w_scales[g][:],
+                in_=grouped[:].rearrange("p c t -> p (c t)"),
+            )
 
         def entries(list_sb, s0, s1):
             return list_sb[:, s0 // LIST_ROWS : s1 // LIST_ROWS]
 
         def gather(picked, g, j, s0, s1):
-            nc.vector.tensor_copy(out=picked[:, s0:s1, j], in_=x_raw[g, j][:].indirect(entries(offs_sb, s0, s1)))
+            nc.vector.tensor_copy(out=picked[:, s0:s1, j], in_=x_raw[g, j].indirect(entries(offs_sb, s0, s1)))
 
         def matmul(g, b, s0, s1):
             nc.tensor.matmul_mx(
                 out=acc[b, s0][:],
-                lhsT=w_mx[g, b][0][:].bitcast(FP8X4),
-                lhsT_scale=w_mx[g, b][1][:],
-                rhs=x_codes[g, s0 // HALF][:, s0 % HALF : s0 % HALF + s1 - s0].bitcast(FP8X4),
+                lhsT=w_codes[g][:, b * P : (b + 1) * P].bitcast(FP8X4),
+                lhsT_scale=w_scales[g][:, b * P : (b + 1) * P],
+                rhs=x_codes[g][:, s0:s1].bitcast(FP8X4),
                 rhs_scale=x_scales[g][:, s0:s1],
                 start=(g == 0),
                 stop=(g == PASSES - 1),
@@ -92,7 +84,7 @@ def tile_picked_kvput_tanh_e_kernel(tc, xT, mem, w1, offs, slot, out):
 
         def quantize_x(g, s0, s1):
             nc.vector.quantize_mx(
-                out=x_codes[g, s0 // HALF][:, s0 % HALF : s0 % HALF + s1 - s0].bitcast(FP8X4),
+                out=x_codes[g][:, s0:s1].bitcast(FP8X4),
                 scales=x_scales[g][:, s0:s1],
                 in_=picked[g][:, s0:s1, :].rearrange("p s t -> p (s t)"),
             )
@@ -106,16 +98,14 @@ def tile_picked_kvput_tanh_e_kernel(tc, xT, mem, w1, offs, slot, out):
         def scatter_scalar(b, s0, s1):
             nc.scalar.activation(window[b][:].indirect(entries(slot_sb, s0, s1)), y[b][:, s0:s1], COPY)
 
-        load_x(0, 0)
+        load_x(0, 0, 2)
         nc.sync.dma_start(offs_sb[:], offs)
-        load_x(0, 1)
-        load_w(0, 0, 2)
-        load_w(1, 1, 2)
-        for g in range(PASSES):
-            for j in range(PACK):
-                if (g, j) not in x_raw:
-                    load_x(g, j)
-        load_w(1, 0, 1)
+        load_x(0, 2, 4)
+        load_x(1, 0, 1)
+        w_raw = sb.tile([P, PASSES, PACK * N], F32, name="w_raw")
+        nc.sync.dma_start(out=w_raw[:], in_=w_rows)
+        for j in range(1, PACK):
+            load_x(1, j, j + 1)
         nc.sync.dma_start(slot_sb[:], slot)
         load_mem(1)
         load_mem(0)
@@ -123,31 +113,28 @@ def tile_picked_kvput_tanh_e_kernel(tc, xT, mem, w1, offs, slot, out):
         pieces = [(1, 0, QUARTER), (1, QUARTER, HALF), (0, 0, HALF), (1, HALF, S), (0, HALF, S)]
         acc = {(b, s0): psum.tile([P, s1 - s0], F32, name="acc%d_%d" % (b, s0)) for b, s0, s1 in pieces}
         picked = [sb.tile([P, S, PACK], BF16, align_bytes=64, name="picked%d" % g) for g in range(PASSES)]
-        x_codes = {
-            (g, h): sb.tile([P, HALF], U32, align_bytes=64, name="x_codes%d%d" % (g, h))
-            for g, h in ((0, 0), (0, 1), (1, 0))
-        }
+        x_codes = [sb.tile([P, S], U32, align_bytes=64, name="x_codes%d" % g) for g in range(PASSES)]
         x_scales = [sb.tile([P, S], U8, align_bytes=64, name="x_scales%d" % g) for g in range(PASSES)]
+        w_codes = [sb.tile([P, N], U32, align_bytes=64, name="w_codes%d" % g) for g in range(PASSES)]
+        w_scales = [sb.tile([P, N], U8, align_bytes=64, name="w_scales%d" % g) for g in range(PASSES)]
         y = [sb.tile([P, S], F32, name="y%d" % b) for b in range(BLOCKS)]
-        w_mx = {(g, b): quantize_w(g, b) for g, b in ((0, 0), (0, 1), (1, 1))}
         for j in range(PACK):
             gather(picked[0], 0, j, 0, S)
-        quantize_x(0, 0, HALF)
-        quantize_x(0, HALF, S)
+        quantize_x(0, 0, S)
+        gather(picked[1], 1, 0, 0, S)
+        for g in range(PASSES):
+            quantize_w(g)
         for b, s0, s1 in pieces:
             matmul(0, b, s0, s1)
         last = PACK - 1
-        for j in range(last):
+        for j in range(1, last):
             gather(picked[1], 1, j, 0, S)
         plain = sb.tile([P, HALF], BF16, name="plain")
         gather(picked[1], 1, last, 0, HALF)
-        nc.scalar.activation(plain[:], x_raw[1, last][:].indirect(entries(offs_sb, HALF, S)), COPY)
+        nc.scalar.activation(plain[:], x_raw[1, last].indirect(entries(offs_sb, HALF, S)), COPY)
         nc.vector.tensor_copy(out=picked[1][:, HALF:S, last], in_=plain[:])
-        for b, s0, s1 in pieces[:2]:
+        for s0, s1 in ((0, QUARTER), (QUARTER, HALF), (HALF, S)):
             quantize_x(1, s0, s1)
-        w_mx[1, 0] = quantize_w(1, 0)
-        x_codes[1, 1] = sb.tile([P, HALF], U32, align_bytes=64, name="x_codes11", tag="w_raw10")
-        quantize_x(1, HALF, S)
         for b, s0, s1 in pieces:
             matmul(1, b, s0, s1)
         tanh(1, 0, QUARTER)
@@ -159,5 +146,5 @@ def tile_picked_kvput_tanh_e_kernel(tc, xT, mem, w1, offs, slot, out):
         scatter_scalar(0, 0, HALF)
         tanh(0, HALF, S)
         scatter_scalar(0, HALF, S)
-        for b in (1, 0):
-            nc.sync.dma_start(out=out[b * P : (b + 1) * P, :], in_=window[b][:])
+        nc.sync.dma_start(out=out[P : 2 * P, :], in_=window[1][:])
+        nc.scalar.dma_start(out=out[0:P, :], in_=window[0][:])

@@ -34,7 +34,7 @@ def tile_picked_kvput_tanh_e_kernel(tc, xT, mem, w1, offs, slot, out):
         offs_sb = lists.tile([P, S // LIST_ROWS], U16, name="offs_sb")
         slot_sb = lists.tile([P, S // LIST_ROWS], U16, name="slot_sb")
         x_rows = xT.rearrange("(g p j) t -> g p j t", g=PASSES, j=PACK)
-        w_rows = w1.rearrange("(g p j) c -> p g (j c)", g=PASSES, j=PACK)
+        w_rows = w1.rearrange("(g p j) c -> g p j c", g=PASSES, j=PACK)
         x_raw = {}
         window = {}
 
@@ -53,16 +53,21 @@ def tile_picked_kvput_tanh_e_kernel(tc, xT, mem, w1, offs, slot, out):
             window[b] = sb.tile([P, U], F32, name="window%d" % b)
             nc.sync.dma_start(out=window[b][:], in_=mem[b * P : (b + 1) * P, :])
 
-        def quantize_w(g):
-            grouped = sb.tile([P, N, PACK], BF16, align_bytes=64, name="w_grouped%d" % g)
+        def load_w(g, j0, j1):
+            raw = sb.tile([P, j1 - j0, N], F32, align_bytes=64, name="w_raw%d%d" % (g, j0))
+            nc.sync.dma_start(out=raw[:], in_=w_rows[g][:, j0:j1, :])
+            return raw
+
+        def group_w(g, b, j0, j1, raw):
             nc.scalar.copy(
-                out=grouped[:].rearrange("p (c i) t -> p c t i", i=4),
-                in_=w_raw[:, g, :].rearrange("p (t c i) -> p c t i", t=PACK, i=4),
+                out=w_grouped[g, b][:, :, j0:j1], in_=raw[:, :, b * P : (b + 1) * P].rearrange("p t c -> p c t")
             )
+
+        def quantize_w(g, b):
             nc.vector.quantize_mx(
-                out=w_codes[g][:].bitcast(FP8X4),
-                scales=w_scales[g][:],
-                in_=grouped[:].rearrange("p c t -> p (c t)"),
+                out=w_codes[g][:, b * P : (b + 1) * P].bitcast(FP8X4),
+                scales=w_scales[g][:, b * P : (b + 1) * P],
+                in_=w_grouped[g, b][:].rearrange("p c t -> p (c t)"),
             )
 
         def entries(list_sb, s0, s1):
@@ -71,12 +76,22 @@ def tile_picked_kvput_tanh_e_kernel(tc, xT, mem, w1, offs, slot, out):
         def gather(picked, g, j, s0, s1):
             nc.vector.tensor_copy(out=picked[:, s0:s1, j], in_=x_raw[g, j].indirect(entries(offs_sb, s0, s1)))
 
+        def gather_plain(plain, g, j, s0, s1):
+            nc.scalar.activation(plain, x_raw[g, j].indirect(entries(offs_sb, s0, s1)), COPY)
+
+        def gather_shared(j, s0):
+            plain = sb.tile([P, S - s0], BF16 if s0 > 0 else F32, name="plain%d" % j)
+            if s0 > 0:
+                gather(picked[1], 1, j, 0, s0)
+            gather_plain(plain[:], 1, j, s0, S)
+            nc.vector.tensor_copy(out=picked[1][:, s0:S, j], in_=plain[:])
+
         def matmul(g, b, s0, s1):
             nc.tensor.matmul_mx(
                 out=acc[b, s0][:],
                 lhsT=w_codes[g][:, b * P : (b + 1) * P].bitcast(FP8X4),
                 lhsT_scale=w_scales[g][:, b * P : (b + 1) * P],
-                rhs=x_codes[g][:, s0:s1].bitcast(FP8X4),
+                rhs=x_codes[g, s0 // HALF][:, s0 % HALF : s0 % HALF + s1 - s0].bitcast(FP8X4),
                 rhs_scale=x_scales[g][:, s0:s1],
                 start=(g == 0),
                 stop=(g == PASSES - 1),
@@ -84,7 +99,7 @@ def tile_picked_kvput_tanh_e_kernel(tc, xT, mem, w1, offs, slot, out):
 
         def quantize_x(g, s0, s1):
             nc.vector.quantize_mx(
-                out=x_codes[g][:, s0:s1].bitcast(FP8X4),
+                out=x_codes[g, s0 // HALF][:, s0 % HALF : s0 % HALF + s1 - s0].bitcast(FP8X4),
                 scales=x_scales[g][:, s0:s1],
                 in_=picked[g][:, s0:s1, :].rearrange("p s t -> p (s t)"),
             )
@@ -98,14 +113,14 @@ def tile_picked_kvput_tanh_e_kernel(tc, xT, mem, w1, offs, slot, out):
         def scatter_scalar(b, s0, s1):
             nc.scalar.activation(window[b][:].indirect(entries(slot_sb, s0, s1)), y[b][:, s0:s1], COPY)
 
-        load_x(0, 0, 2)
+        load_x(0, 0, PACK)
         nc.sync.dma_start(offs_sb[:], offs)
-        load_x(0, 2, 4)
-        load_x(1, 0, 1)
-        w_raw = sb.tile([P, PASSES, PACK * N], F32, name="w_raw")
-        nc.sync.dma_start(out=w_raw[:], in_=w_rows)
-        for j in range(1, PACK):
-            load_x(1, j, j + 1)
+        w_pass0 = load_w(0, 0, PACK)
+        w_early = load_w(1, 0, PACK // 2)
+        load_x(1, 0, 2)
+        load_x(1, 2, 3)
+        load_x(1, 3, 4)
+        w_late = load_w(1, PACK // 2, PACK)
         nc.sync.dma_start(slot_sb[:], slot)
         load_mem(1)
         load_mem(0)
@@ -113,28 +128,44 @@ def tile_picked_kvput_tanh_e_kernel(tc, xT, mem, w1, offs, slot, out):
         pieces = [(1, 0, QUARTER), (1, QUARTER, HALF), (0, 0, HALF), (1, HALF, S), (0, HALF, S)]
         acc = {(b, s0): psum.tile([P, s1 - s0], F32, name="acc%d_%d" % (b, s0)) for b, s0, s1 in pieces}
         picked = [sb.tile([P, S, PACK], BF16, align_bytes=64, name="picked%d" % g) for g in range(PASSES)]
-        x_codes = [sb.tile([P, S], U32, align_bytes=64, name="x_codes%d" % g) for g in range(PASSES)]
+        x_codes = {
+            (g, h): sb.tile([P, HALF], U32, align_bytes=64, name="x_codes%d%d" % (g, h))
+            for g, h in ((0, 0), (0, 1), (1, 0))
+        }
         x_scales = [sb.tile([P, S], U8, align_bytes=64, name="x_scales%d" % g) for g in range(PASSES)]
         w_codes = [sb.tile([P, N], U32, align_bytes=64, name="w_codes%d" % g) for g in range(PASSES)]
         w_scales = [sb.tile([P, N], U8, align_bytes=64, name="w_scales%d" % g) for g in range(PASSES)]
+        w_grouped = {
+            (g, b): sb.tile([P, P, PACK], BF16, align_bytes=64, name="w_grouped%d%d" % (g, b))
+            for g in range(PASSES)
+            for b in range(BLOCKS)
+        }
         y = [sb.tile([P, S], F32, name="y%d" % b) for b in range(BLOCKS)]
-        for j in range(PACK):
+        pair = sb.tile([P, 2, S], F32, name="pair")
+        for j in range(2):
             gather(picked[0], 0, j, 0, S)
-        quantize_x(0, 0, S)
-        gather(picked[1], 1, 0, 0, S)
-        for g in range(PASSES):
-            quantize_w(g)
+            gather_plain(pair[:, j, :], 0, 2 + j, 0, S)
+        nc.scalar.copy(out=picked[0][:, :, 2:PACK], in_=pair[:].rearrange("p t s -> p s t"))
+        quantize_x(0, 0, HALF)
+        quantize_x(0, HALF, S)
+        for b in range(BLOCKS):
+            group_w(0, b, 0, PACK, w_pass0)
+            quantize_w(0, b)
+            group_w(1, b, 0, PACK // 2, w_early)
         for b, s0, s1 in pieces:
             matmul(0, b, s0, s1)
-        last = PACK - 1
-        for j in range(1, last):
-            gather(picked[1], 1, j, 0, S)
-        plain = sb.tile([P, HALF], BF16, name="plain")
-        gather(picked[1], 1, last, 0, HALF)
-        nc.scalar.activation(plain[:], x_raw[1, last].indirect(entries(offs_sb, HALF, S)), COPY)
-        nc.vector.tensor_copy(out=picked[1][:, HALF:S, last], in_=plain[:])
-        for s0, s1 in ((0, QUARTER), (QUARTER, HALF), (HALF, S)):
-            quantize_x(1, s0, s1)
+        gather(picked[1], 1, 0, 0, S)
+        gather_shared(1, 0)
+        gather_shared(2, HALF)
+        gather_shared(3, HALF)
+        for b in (1, 0):
+            group_w(1, b, PACK // 2, PACK, w_late)
+        quantize_x(1, 0, QUARTER)
+        quantize_w(1, 1)
+        quantize_x(1, QUARTER, HALF)
+        quantize_w(1, 0)
+        x_codes[1, 1] = sb.tile([P, HALF], U32, align_bytes=64, name="x_codes11", tag="w_raw12")
+        quantize_x(1, HALF, S)
         for b, s0, s1 in pieces:
             matmul(1, b, s0, s1)
         tanh(1, 0, QUARTER)

@@ -44,7 +44,7 @@ def tile_picked_kvput_tanh_e_kernel(tc, xT, mem, w1, offs, slot, out):
         nc.scalar.activation(warm_out[:], warm[:], TANH)
 
         def load_x(g, j0, j1):
-            raw = sb.tile([P, j1 - j0, T], F32, name="x_raw%d%d" % (g, j0))
+            raw = sb.tile([P, j1 - j0, T], F32, align_bytes=64, name="x_raw%d%d" % (g, j0))
             nc.sync.dma_start(out=raw[:], in_=x_rows[g][:, j0:j1, :])
             for j in range(j0, j1):
                 x_raw[g, j] = raw[:, j - j0, :]
@@ -122,15 +122,15 @@ def tile_picked_kvput_tanh_e_kernel(tc, xT, mem, w1, offs, slot, out):
         load_x(1, 3, 4)
         w_late = load_w(1, PACK // 2, PACK)
         nc.sync.dma_start(slot_sb[:], slot)
-        load_mem(1)
         load_mem(0)
+        load_mem(1)
 
-        pieces = [(1, 0, QUARTER), (1, QUARTER, HALF), (0, 0, HALF), (1, HALF, S), (0, HALF, S)]
+        pieces = [(0, 0, QUARTER), (0, QUARTER, HALF), (1, 0, HALF), (0, HALF, S), (1, HALF, S)]
         acc = {(b, s0): psum.tile([P, s1 - s0], F32, name="acc%d_%d" % (b, s0)) for b, s0, s1 in pieces}
         picked = [sb.tile([P, S, PACK], BF16, align_bytes=64, name="picked%d" % g) for g in range(PASSES)]
         x_codes = {
             (g, h): sb.tile([P, HALF], U32, align_bytes=64, name="x_codes%d%d" % (g, h))
-            for g, h in ((0, 0), (0, 1), (1, 0))
+            for g, h in ((0, 0), (0, 1))
         }
         x_scales = [sb.tile([P, S], U8, align_bytes=64, name="x_scales%d" % g) for g in range(PASSES)]
         w_codes = [sb.tile([P, N], U32, align_bytes=64, name="w_codes%d" % g) for g in range(PASSES)]
@@ -158,24 +158,21 @@ def tile_picked_kvput_tanh_e_kernel(tc, xT, mem, w1, offs, slot, out):
         gather_shared(1, 0)
         gather_shared(2, HALF)
         gather_shared(3, HALF)
-        for b in (1, 0):
+        for b in range(BLOCKS):
             group_w(1, b, PACK // 2, PACK, w_late)
+        x_codes[1, 0] = sb.tile([P, HALF], U32, align_bytes=64, name="x_codes10", tag="x_raw13")
         quantize_x(1, 0, QUARTER)
-        quantize_w(1, 1)
-        quantize_x(1, QUARTER, HALF)
         quantize_w(1, 0)
+        quantize_x(1, QUARTER, HALF)
+        quantize_w(1, 1)
         x_codes[1, 1] = sb.tile([P, HALF], U32, align_bytes=64, name="x_codes11", tag="w_raw12")
         quantize_x(1, HALF, S)
         for b, s0, s1 in pieces:
             matmul(1, b, s0, s1)
-        tanh(1, 0, QUARTER)
-        scatter_vector(1, 0, QUARTER)
-        tanh(1, QUARTER, HALF)
-        tanh(0, 0, HALF)
-        tanh(1, HALF, S)
-        scatter_vector(1, QUARTER, S)
-        scatter_scalar(0, 0, HALF)
-        tanh(0, HALF, S)
-        scatter_scalar(0, HALF, S)
-        nc.sync.dma_start(out=out[P : 2 * P, :], in_=window[1][:])
-        nc.scalar.dma_start(out=out[0:P, :], in_=window[0][:])
+        for piece in pieces:
+            tanh(*piece)
+        scatter_vector(0, 0, QUARTER)
+        scatter_vector(1, 0, S)
+        scatter_scalar(0, QUARTER, S)
+        for b in range(BLOCKS):
+            nc.sync.dma_start(out=out[b * P : (b + 1) * P, :], in_=window[b][:])

@@ -60,7 +60,8 @@ def tile_picked_kvput_tanh_e_kernel(tc, xT, mem, w1, offs, slot, out):
 
         def group_w(g, b, j0, j1, raw):
             nc.scalar.copy(
-                out=w_grouped[g, b][:, :, j0:j1], in_=raw[:, :, b * P : (b + 1) * P].rearrange("p t c -> p c t")
+                out=w_grouped[g, b][:].rearrange("p (c i) t -> p c t i", i=4),
+                in_=raw[:, :, b * P : (b + 1) * P].rearrange("p t (c i) -> p c t i", i=4),
             )
 
         def quantize_w(g, b):
@@ -91,7 +92,7 @@ def tile_picked_kvput_tanh_e_kernel(tc, xT, mem, w1, offs, slot, out):
                 out=acc[b, s0][:],
                 lhsT=w_codes[g][:, b * P : (b + 1) * P].bitcast(FP8X4),
                 lhsT_scale=w_scales[g][:, b * P : (b + 1) * P],
-                rhs=x_codes[g, s0 // HALF][:, s0 % HALF : s0 % HALF + s1 - s0].bitcast(FP8X4),
+                rhs=x_codes[g][:, s0:s1].bitcast(FP8X4),
                 rhs_scale=x_scales[g][:, s0:s1],
                 start=(g == 0),
                 stop=(g == PASSES - 1),
@@ -99,7 +100,7 @@ def tile_picked_kvput_tanh_e_kernel(tc, xT, mem, w1, offs, slot, out):
 
         def quantize_x(g, s0, s1):
             nc.vector.quantize_mx(
-                out=x_codes[g, s0 // HALF][:, s0 % HALF : s0 % HALF + s1 - s0].bitcast(FP8X4),
+                out=x_codes[g][:, s0:s1].bitcast(FP8X4),
                 scales=x_scales[g][:, s0:s1],
                 in_=picked[g][:, s0:s1, :].rearrange("p s t -> p (s t)"),
             )
@@ -116,22 +117,18 @@ def tile_picked_kvput_tanh_e_kernel(tc, xT, mem, w1, offs, slot, out):
         load_x(0, 0, PACK)
         nc.sync.dma_start(offs_sb[:], offs)
         w_pass0 = load_w(0, 0, PACK)
-        w_early = load_w(1, 0, PACK // 2)
         load_x(1, 0, 2)
         load_x(1, 2, 3)
         load_x(1, 3, 4)
-        w_late = load_w(1, PACK // 2, PACK)
+        w_late = load_w(1, 0, PACK)
         nc.sync.dma_start(slot_sb[:], slot)
         load_mem(0)
         load_mem(1)
 
-        pieces = [(0, 0, QUARTER), (0, QUARTER, HALF), (1, 0, HALF), (0, HALF, S), (1, HALF, S)]
+        pieces = [(0, 0, QUARTER), (0, QUARTER, HALF), (0, HALF, S), (1, 0, HALF), (1, HALF, S)]
         acc = {(b, s0): psum.tile([P, s1 - s0], F32, name="acc%d_%d" % (b, s0)) for b, s0, s1 in pieces}
         picked = [sb.tile([P, S, PACK], BF16, align_bytes=64, name="picked%d" % g) for g in range(PASSES)]
-        x_codes = {
-            (g, h): sb.tile([P, HALF], U32, align_bytes=64, name="x_codes%d%d" % (g, h))
-            for g, h in ((0, 0), (0, 1))
-        }
+        x_codes = [sb.tile([P, S], U32, align_bytes=64, name="x_codes0")]
         x_scales = [sb.tile([P, S], U8, align_bytes=64, name="x_scales%d" % g) for g in range(PASSES)]
         w_codes = [sb.tile([P, N], U32, align_bytes=64, name="w_codes%d" % g) for g in range(PASSES)]
         w_scales = [sb.tile([P, N], U8, align_bytes=64, name="w_scales%d" % g) for g in range(PASSES)]
@@ -146,12 +143,10 @@ def tile_picked_kvput_tanh_e_kernel(tc, xT, mem, w1, offs, slot, out):
             gather(picked[0], 0, j, 0, S)
             gather_plain(pair[:, j, :], 0, 2 + j, 0, S)
         nc.scalar.copy(out=picked[0][:, :, 2:PACK], in_=pair[:].rearrange("p t s -> p s t"))
-        quantize_x(0, 0, HALF)
-        quantize_x(0, HALF, S)
+        quantize_x(0, 0, S)
         for b in range(BLOCKS):
             group_w(0, b, 0, PACK, w_pass0)
             quantize_w(0, b)
-            group_w(1, b, 0, PACK // 2, w_early)
         for b, s0, s1 in pieces:
             matmul(0, b, s0, s1)
         gather(picked[1], 1, 0, 0, S)
@@ -159,14 +154,12 @@ def tile_picked_kvput_tanh_e_kernel(tc, xT, mem, w1, offs, slot, out):
         gather_shared(2, HALF)
         gather_shared(3, HALF)
         for b in range(BLOCKS):
-            group_w(1, b, PACK // 2, PACK, w_late)
-        x_codes[1, 0] = sb.tile([P, HALF], U32, align_bytes=64, name="x_codes10", tag="x_raw13")
-        quantize_x(1, 0, QUARTER)
-        quantize_w(1, 0)
-        quantize_x(1, QUARTER, HALF)
-        quantize_w(1, 1)
-        x_codes[1, 1] = sb.tile([P, HALF], U32, align_bytes=64, name="x_codes11", tag="w_raw12")
-        quantize_x(1, HALF, S)
+            group_w(1, b, 0, PACK, w_late)
+        x_codes.append(sb.tile([P, S], U32, align_bytes=64, name="x_codes1", tag="x_raw13"))
+        for s0, s1 in ((0, HALF), (HALF, S)):
+            quantize_x(1, s0, s1)
+        for b in range(BLOCKS):
+            quantize_w(1, b)
         for b, s0, s1 in pieces:
             matmul(1, b, s0, s1)
         for piece in pieces:

@@ -105,8 +105,8 @@ def tile_picked_kvput_tanh_e_kernel(tc, xT, mem, w1, offs, slot, out):
                 in_=picked[g][:, s0:s1, :].rearrange("p s t -> p (s t)"),
             )
 
-        def tanh(b, s0, s1):
-            nc.scalar.activation(y[b][:, s0:s1], acc[b, s0][:], TANH)
+        def tanh(b, s0, s1, base):
+            nc.scalar.activation(y[b][:, s0:s1], acc[b, base][:, s0 - base : s1 - base], TANH)
 
         def scatter_vector(b, s0, s1):
             nc.vector.tensor_copy(out=window[b][:].indirect(entries(slot_sb, s0, s1)), in_=y[b][:, s0:s1])
@@ -122,10 +122,10 @@ def tile_picked_kvput_tanh_e_kernel(tc, xT, mem, w1, offs, slot, out):
         load_x(1, 3, 4)
         w_late = load_w(1, 0, PACK)
         nc.sync.dma_start(slot_sb[:], slot)
-        load_mem(0)
         load_mem(1)
+        load_mem(0)
 
-        pieces = [(0, 0, QUARTER), (0, QUARTER, HALF), (0, HALF, S), (1, 0, HALF), (1, HALF, S)]
+        pieces = [(1, 0, QUARTER), (1, QUARTER, HALF), (1, HALF, S), (0, 0, HALF), (0, HALF, S)]
         acc = {(b, s0): psum.tile([P, s1 - s0], F32, name="acc%d_%d" % (b, s0)) for b, s0, s1 in pieces}
         picked = [sb.tile([P, S, PACK], BF16, align_bytes=64, name="picked%d" % g) for g in range(PASSES)]
         x_codes = [sb.tile([P, S], U32, align_bytes=64, name="x_codes0")]
@@ -153,19 +153,22 @@ def tile_picked_kvput_tanh_e_kernel(tc, xT, mem, w1, offs, slot, out):
         gather_shared(1, 0)
         gather_shared(2, HALF)
         gather_shared(3, HALF)
-        for b in range(BLOCKS):
+        for b in (1, 0):
             group_w(1, b, 0, PACK, w_late)
         x_codes.append(sb.tile([P, S], U32, align_bytes=64, name="x_codes1", tag="x_raw13"))
         for s0, s1 in ((0, HALF), (HALF, S)):
             quantize_x(1, s0, s1)
-        for b in range(BLOCKS):
+        for b in (1, 0):
             quantize_w(1, b)
         for b, s0, s1 in pieces:
             matmul(1, b, s0, s1)
-        for piece in pieces:
-            tanh(*piece)
-        scatter_vector(0, 0, QUARTER)
-        scatter_vector(1, 0, S)
-        scatter_scalar(0, QUARTER, S)
-        for b in range(BLOCKS):
+        for b, s0, s1 in pieces[:-1]:
+            tanh(b, s0, s1, s0)
+        tanh(0, HALF, S - QUARTER, HALF)
+        tanh(0, S - QUARTER, S, HALF)
+        scatter_vector(1, 0, QUARTER)
+        scatter_vector(1, QUARTER, S)
+        scatter_scalar(0, 0, S - QUARTER)
+        scatter_vector(0, S - QUARTER, S)
+        for b in (1, 0):
             nc.sync.dma_start(out=out[b * P : (b + 1) * P, :], in_=window[b][:])

@@ -22,6 +22,7 @@ BLOCKS = N // P
 HALF = S // 2
 QUARTER = S // 4
 LIST_ROWS = 16
+FIRST, SECOND = 0, 1
 
 
 def tile_picked_kvput_tanh_e_kernel(tc, xT, mem, w1, offs, slot, out):
@@ -36,6 +37,7 @@ def tile_picked_kvput_tanh_e_kernel(tc, xT, mem, w1, offs, slot, out):
         x_rows = xT.rearrange("(g p j) t -> g p j t", g=PASSES, j=PACK)
         w_rows = w1.rearrange("(g p j) c -> g p j c", g=PASSES, j=PACK)
         x_raw = {}
+        w_raw = {}
         window = {}
 
         warm = sb.tile([P, 1], F32, name="warm")
@@ -53,29 +55,35 @@ def tile_picked_kvput_tanh_e_kernel(tc, xT, mem, w1, offs, slot, out):
             window[b] = sb.tile([P, U], F32, name="window%d" % b)
             nc.sync.dma_start(out=window[b][:], in_=mem[b * P : (b + 1) * P, :])
 
-        def load_w(g, j0, j1):
-            raw = sb.tile([P, j1 - j0, N], F32, align_bytes=64, name="w_raw%d%d" % (g, j0))
-            nc.sync.dma_start(out=raw[:], in_=w_rows[g][:, j0:j1, :])
-            return raw
+        def load_w(g, b):
+            raw = sb.tile([P, PACK, P], F32, align_bytes=64, name="w_raw%d%d" % (g, b))
+            nc.sync.dma_start(out=raw[:], in_=w_rows[g][:, :, b * P : (b + 1) * P])
+            w_raw[g, b] = raw[:]
 
-        def group_w(g, b, j0, j1, raw):
+        def load_w_pass(g):
+            raw = sb.tile([P, PACK, N], F32, align_bytes=64, name="w_raw%d" % g)
+            nc.sync.dma_start(out=raw[:], in_=w_rows[g])
+            for b in range(BLOCKS):
+                w_raw[g, b] = raw[:, :, b * P : (b + 1) * P]
+
+        def group_w(g, b):
             nc.scalar.copy(
                 out=w_grouped[g, b][:].rearrange("p (c i) t -> p c t i", i=4),
-                in_=raw[:, :, b * P : (b + 1) * P].rearrange("p t (c i) -> p c t i", i=4),
+                in_=w_raw[g, b].rearrange("p t (c i) -> p c t i", i=4),
             )
 
         def quantize_w(g, b):
             nc.vector.quantize_mx(
-                out=w_codes[g][:, b * P : (b + 1) * P].bitcast(FP8X4),
-                scales=w_scales[g][:, b * P : (b + 1) * P],
+                out=w_codes[g, b][:].bitcast(FP8X4),
+                scales=w_scales[g, b][:],
                 in_=w_grouped[g, b][:].rearrange("p c t -> p (c t)"),
             )
 
         def entries(list_sb, s0, s1):
             return list_sb[:, s0 // LIST_ROWS : s1 // LIST_ROWS]
 
-        def gather(picked, g, j, s0, s1):
-            nc.vector.tensor_copy(out=picked[:, s0:s1, j], in_=x_raw[g, j].indirect(entries(offs_sb, s0, s1)))
+        def gather(g, j, s0, s1):
+            nc.vector.tensor_copy(out=picked[g][:, s0:s1, j], in_=x_raw[g, j].indirect(entries(offs_sb, s0, s1)))
 
         def gather_plain(plain, g, j, s0, s1):
             nc.scalar.activation(plain, x_raw[g, j].indirect(entries(offs_sb, s0, s1)), COPY)
@@ -83,16 +91,20 @@ def tile_picked_kvput_tanh_e_kernel(tc, xT, mem, w1, offs, slot, out):
         def gather_shared(j, s0):
             plain = sb.tile([P, S - s0], BF16 if s0 > 0 else F32, name="plain%d" % j)
             if s0 > 0:
-                gather(picked[1], 1, j, 0, s0)
+                gather(1, j, 0, s0)
             gather_plain(plain[:], 1, j, s0, S)
             nc.vector.tensor_copy(out=picked[1][:, s0:S, j], in_=plain[:])
+
+        def codes(g, s0, s1):
+            tile, base = x_codes[g, s0 // HALF]
+            return tile[:, s0 - base : s1 - base]
 
         def matmul(g, b, s0, s1):
             nc.tensor.matmul_mx(
                 out=acc[b, s0][:],
-                lhsT=w_codes[g][:, b * P : (b + 1) * P].bitcast(FP8X4),
-                lhsT_scale=w_scales[g][:, b * P : (b + 1) * P],
-                rhs=x_codes[g][:, s0:s1].bitcast(FP8X4),
+                lhsT=w_codes[g, b][:].bitcast(FP8X4),
+                lhsT_scale=w_scales[g, b][:],
+                rhs=codes(g, s0, s1).bitcast(FP8X4),
                 rhs_scale=x_scales[g][:, s0:s1],
                 start=(g == 0),
                 stop=(g == PASSES - 1),
@@ -100,7 +112,7 @@ def tile_picked_kvput_tanh_e_kernel(tc, xT, mem, w1, offs, slot, out):
 
         def quantize_x(g, s0, s1):
             nc.vector.quantize_mx(
-                out=x_codes[g][:, s0:s1].bitcast(FP8X4),
+                out=codes(g, s0, s1).bitcast(FP8X4),
                 scales=x_scales[g][:, s0:s1],
                 in_=picked[g][:, s0:s1, :].rearrange("p s t -> p (s t)"),
             )
@@ -116,59 +128,60 @@ def tile_picked_kvput_tanh_e_kernel(tc, xT, mem, w1, offs, slot, out):
 
         load_x(0, 0, PACK)
         nc.sync.dma_start(offs_sb[:], offs)
-        w_pass0 = load_w(0, 0, PACK)
+        load_w_pass(0)
         load_x(1, 0, 2)
         load_x(1, 2, 3)
         load_x(1, 3, 4)
-        w_late = load_w(1, 0, PACK)
+        load_w(1, FIRST)
+        load_w(1, SECOND)
         nc.sync.dma_start(slot_sb[:], slot)
-        load_mem(1)
-        load_mem(0)
+        load_mem(FIRST)
+        load_mem(SECOND)
 
-        pieces = [(1, 0, QUARTER), (1, QUARTER, HALF), (1, HALF, S), (0, 0, HALF), (0, HALF, S)]
-        acc = {(b, s0): psum.tile([P, s1 - s0], F32, name="acc%d_%d" % (b, s0)) for b, s0, s1 in pieces}
+        first_pieces = [(FIRST, 0, QUARTER), (FIRST, QUARTER, HALF), (FIRST, HALF, S)]
+        second_pieces = [(SECOND, 0, HALF), (SECOND, HALF, S)]
+        acc = {(b, s0): psum.tile([P, s1 - s0], F32, name="acc%d_%d" % (b, s0)) for b, s0, s1 in first_pieces + second_pieces}
         picked = [sb.tile([P, S, PACK], BF16, align_bytes=64, name="picked%d" % g) for g in range(PASSES)]
-        x_codes = [sb.tile([P, S], U32, align_bytes=64, name="x_codes0")]
+        codes0 = sb.tile([P, S], U32, align_bytes=64, name="x_codes0")
+        x_codes = {(0, h): (codes0, 0) for h in range(2)}
         x_scales = [sb.tile([P, S], U8, align_bytes=64, name="x_scales%d" % g) for g in range(PASSES)]
-        w_codes = [sb.tile([P, N], U32, align_bytes=64, name="w_codes%d" % g) for g in range(PASSES)]
-        w_scales = [sb.tile([P, N], U8, align_bytes=64, name="w_scales%d" % g) for g in range(PASSES)]
-        w_grouped = {
-            (g, b): sb.tile([P, P, PACK], BF16, align_bytes=64, name="w_grouped%d%d" % (g, b))
-            for g in range(PASSES)
-            for b in range(BLOCKS)
-        }
+        both = [(g, b) for g in range(PASSES) for b in range(BLOCKS)]
+        w_codes = {gb: sb.tile([P, P], U32, align_bytes=64, name="w_codes%d%d" % gb) for gb in both}
+        w_scales = {gb: sb.tile([P, P], U8, align_bytes=64, name="w_scales%d%d" % gb) for gb in both}
+        w_grouped = {gb: sb.tile([P, P, PACK], BF16, align_bytes=64, name="w_grouped%d%d" % gb) for gb in both}
         y = [sb.tile([P, S], F32, name="y%d" % b) for b in range(BLOCKS)]
         pair = sb.tile([P, 2, S], F32, name="pair")
         for j in range(2):
-            gather(picked[0], 0, j, 0, S)
+            gather(0, j, 0, S)
             gather_plain(pair[:, j, :], 0, 2 + j, 0, S)
         nc.scalar.copy(out=picked[0][:, :, 2:PACK], in_=pair[:].rearrange("p t s -> p s t"))
         quantize_x(0, 0, S)
         for b in range(BLOCKS):
-            group_w(0, b, 0, PACK, w_pass0)
+            group_w(0, b)
             quantize_w(0, b)
-        for b, s0, s1 in pieces:
+        for b, s0, s1 in first_pieces + second_pieces:
             matmul(0, b, s0, s1)
-        gather(picked[1], 1, 0, 0, S)
+        gather(1, 0, 0, S)
         gather_shared(1, 0)
         gather_shared(2, HALF)
         gather_shared(3, HALF)
-        for b in (1, 0):
-            group_w(1, b, 0, PACK, w_late)
-        x_codes.append(sb.tile([P, S], U32, align_bytes=64, name="x_codes1", tag="x_raw13"))
-        for s0, s1 in ((0, HALF), (HALF, S)):
-            quantize_x(1, s0, s1)
-        for b in (1, 0):
-            quantize_w(1, b)
-        for b, s0, s1 in pieces:
+        for b in range(BLOCKS):
+            group_w(1, b)
+        x_codes[1, 0] = (sb.tile([P, HALF], U32, align_bytes=64, name="x_codes10", tag="x_raw13"), 0)
+        x_codes[1, 1] = (sb.tile([P, HALF], U32, align_bytes=64, name="x_codes11", tag="w_raw1%d" % FIRST), HALF)
+        quantize_x(1, 0, HALF)
+        quantize_w(1, FIRST)
+        quantize_x(1, HALF, S)
+        quantize_w(1, SECOND)
+        for b, s0, s1 in first_pieces + second_pieces:
             matmul(1, b, s0, s1)
-        for b, s0, s1 in pieces[:-1]:
+        for b, s0, s1 in first_pieces + second_pieces[:1]:
             tanh(b, s0, s1, s0)
-        tanh(0, HALF, S - QUARTER, HALF)
-        tanh(0, S - QUARTER, S, HALF)
-        scatter_vector(1, 0, QUARTER)
-        scatter_vector(1, QUARTER, S)
-        scatter_scalar(0, 0, S - QUARTER)
-        scatter_vector(0, S - QUARTER, S)
-        for b in (1, 0):
+        tanh(SECOND, HALF, S - QUARTER, HALF)
+        tanh(SECOND, S - QUARTER, S, HALF)
+        scatter_vector(FIRST, 0, QUARTER)
+        scatter_vector(FIRST, QUARTER, S)
+        scatter_scalar(SECOND, 0, S - QUARTER)
+        scatter_vector(SECOND, S - QUARTER, S)
+        for b in (FIRST, SECOND):
             nc.sync.dma_start(out=out[b * P : (b + 1) * P, :], in_=window[b][:])

@@ -89,9 +89,8 @@ def tile_picked_kvput_tanh_e_kernel(tc, xT, mem, w1, offs, slot, out):
             nc.scalar.activation(plain, x_raw[g, j].indirect(entries(offs_sb, s0, s1)), COPY)
 
         def gather_shared(j, s0):
-            plain = sb.tile([P, S - s0], BF16 if s0 > 0 else F32, name="plain%d" % j)
-            if s0 > 0:
-                gather(1, j, 0, s0)
+            plain = sb.tile([P, S - s0], BF16, name="plain%d" % j)
+            gather(1, j, 0, s0)
             gather_plain(plain[:], 1, j, s0, S)
             nc.vector.tensor_copy(out=picked[1][:, s0:S, j], in_=plain[:])
 
@@ -154,15 +153,21 @@ def tile_picked_kvput_tanh_e_kernel(tc, xT, mem, w1, offs, slot, out):
         for j in range(2):
             gather(0, j, 0, S)
             gather_plain(pair[:, j, :], 0, 2 + j, 0, S)
-        nc.scalar.copy(out=picked[0][:, :, 2:PACK], in_=pair[:].rearrange("p t s -> p s t"))
-        quantize_x(0, 0, S)
+        nc.vector.tensor_copy(out=picked[0][:, :, 2:PACK], in_=pair[:].rearrange("p t s -> p s t"))
         for b in range(BLOCKS):
             group_w(0, b)
             quantize_w(0, b)
+        quantize_x(0, 0, S)
         for b, s0, s1 in first_pieces + second_pieces:
             matmul(0, b, s0, s1)
-        gather(1, 0, 0, S)
-        gather_shared(1, 0)
+        row1 = sb.tile([P, HALF], F32, name="row1")
+        pair1 = sb.tile([P, 2, HALF], F32, name="pair1")
+        gather(1, 0, 0, HALF)
+        gather_plain(row1[:], 1, 1, 0, HALF)
+        for j in range(2):
+            gather_plain(pair1[:, j, :], 1, j, HALF, S)
+        nc.vector.tensor_copy(out=picked[1][:, 0:HALF, 1], in_=row1[:])
+        nc.vector.tensor_copy(out=picked[1][:, HALF:S, 0:2], in_=pair1[:].rearrange("p t s -> p s t"))
         gather_shared(2, HALF)
         gather_shared(3, HALF)
         for b in range(BLOCKS):

@@ -23,6 +23,7 @@ HALF = S // 2
 QUARTER = S // 4
 LIST_ROWS = 16
 FIRST, SECOND = 0, 1
+LENT = 192
 
 
 def tile_picked_kvput_tanh_e_kernel(tc, xT, mem, w1, offs, slot, out):
@@ -66,8 +67,8 @@ def tile_picked_kvput_tanh_e_kernel(tc, xT, mem, w1, offs, slot, out):
             for b in range(BLOCKS):
                 w_raw[g, b] = raw[:, :, b * P : (b + 1) * P]
 
-        def group_w(g, b):
-            nc.scalar.copy(
+        def group_w(g, b, copy):
+            copy(
                 out=w_grouped[g, b][:].rearrange("p (c i) t -> p c t i", i=4),
                 in_=w_raw[g, b].rearrange("p t (c i) -> p c t i", i=4),
             )
@@ -127,10 +128,10 @@ def tile_picked_kvput_tanh_e_kernel(tc, xT, mem, w1, offs, slot, out):
 
         load_x(0, 0, PACK)
         nc.sync.dma_start(offs_sb[:], offs)
-        load_w_pass(0)
         load_x(1, 0, 2)
         load_x(1, 2, 3)
         load_x(1, 3, 4)
+        load_w_pass(0)
         load_w(1, FIRST)
         load_w(1, SECOND)
         nc.sync.dma_start(slot_sb[:], slot)
@@ -139,7 +140,7 @@ def tile_picked_kvput_tanh_e_kernel(tc, xT, mem, w1, offs, slot, out):
 
         first_pieces = [(FIRST, 0, QUARTER), (FIRST, QUARTER, HALF), (FIRST, HALF, S)]
         second_pieces = [(SECOND, 0, HALF), (SECOND, HALF, S)]
-        acc = {(b, s0): psum.tile([P, s1 - s0], F32, name="acc%d_%d" % (b, s0)) for b, s0, s1 in first_pieces + second_pieces}
+        acc = {(b, s0): psum.tile([P, s1 - s0], F32, name="acc%d_%d" % (b, s0)) for b, s0, s1 in first_pieces[:2] + second_pieces}
         picked = [sb.tile([P, S, PACK], BF16, align_bytes=64, name="picked%d" % g) for g in range(PASSES)]
         codes0 = sb.tile([P, S], U32, align_bytes=64, name="x_codes0")
         x_codes = {(0, h): (codes0, 0) for h in range(2)}
@@ -148,18 +149,12 @@ def tile_picked_kvput_tanh_e_kernel(tc, xT, mem, w1, offs, slot, out):
         w_codes = {gb: sb.tile([P, P], U32, align_bytes=64, name="w_codes%d%d" % gb) for gb in both}
         w_scales = {gb: sb.tile([P, P], U8, align_bytes=64, name="w_scales%d%d" % gb) for gb in both}
         w_grouped = {gb: sb.tile([P, P, PACK], BF16, align_bytes=64, name="w_grouped%d%d" % gb) for gb in both}
-        y = [sb.tile([P, S], F32, name="y%d" % b) for b in range(BLOCKS)]
         pair = sb.tile([P, 2, S], F32, name="pair")
         for j in range(2):
             gather(0, j, 0, S)
             gather_plain(pair[:, j, :], 0, 2 + j, 0, S)
         nc.vector.tensor_copy(out=picked[0][:, :, 2:PACK], in_=pair[:].rearrange("p t s -> p s t"))
-        for b in range(BLOCKS):
-            group_w(0, b)
-            quantize_w(0, b)
         quantize_x(0, 0, S)
-        for b, s0, s1 in first_pieces + second_pieces:
-            matmul(0, b, s0, s1)
         row1 = sb.tile([P, HALF], F32, name="row1")
         pair1 = sb.tile([P, 2, HALF], F32, name="pair1")
         gather(1, 0, 0, HALF)
@@ -170,23 +165,31 @@ def tile_picked_kvput_tanh_e_kernel(tc, xT, mem, w1, offs, slot, out):
         nc.vector.tensor_copy(out=picked[1][:, HALF:S, 0:2], in_=pair1[:].rearrange("p t s -> p s t"))
         gather_shared(2, HALF)
         gather_shared(3, HALF)
-        for b in range(BLOCKS):
-            group_w(1, b)
         x_codes[1, 0] = (sb.tile([P, HALF], U32, align_bytes=64, name="x_codes10", tag="x_raw13"), 0)
-        x_codes[1, 1] = (sb.tile([P, HALF], U32, align_bytes=64, name="x_codes11", tag="w_raw1%d" % FIRST), HALF)
+        x_codes[1, 1] = (sb.tile([P, HALF], U32, align_bytes=64, name="x_codes11"), HALF)
         quantize_x(1, 0, HALF)
-        quantize_w(1, FIRST)
         quantize_x(1, HALF, S)
+        for b in range(BLOCKS):
+            group_w(0, b, nc.scalar.copy)
+        quantize_w(0, FIRST)
+        group_w(1, FIRST, nc.vector.tensor_copy)
+        quantize_w(0, SECOND)
+        quantize_w(1, FIRST)
+        group_w(1, SECOND, nc.scalar.copy)
         quantize_w(1, SECOND)
-        for b, s0, s1 in first_pieces + second_pieces:
-            matmul(1, b, s0, s1)
-        for b, s0, s1 in first_pieces + second_pieces[:1]:
+        y = {
+            FIRST: sb.tile([P, S], F32, align_bytes=64, name="y_first", tag="w_raw1%d" % SECOND),
+            SECOND: sb.tile([P, S], F32, name="y_second"),
+        }
+        pieces = first_pieces[:2] + second_pieces + first_pieces[2:]
+        for b, s0, s1 in pieces:
+            if (b, s0) not in acc:
+                acc[b, s0] = psum.tile([P, s1 - s0], F32, name="acc_last", tag="acc%d_%d" % (FIRST, QUARTER))
+            for g in range(PASSES):
+                matmul(g, b, s0, s1)
             tanh(b, s0, s1, s0)
-        tanh(SECOND, HALF, S - QUARTER, HALF)
-        tanh(SECOND, S - QUARTER, S, HALF)
-        scatter_vector(FIRST, 0, QUARTER)
-        scatter_vector(FIRST, QUARTER, S)
-        scatter_scalar(SECOND, 0, S - QUARTER)
-        scatter_vector(SECOND, S - QUARTER, S)
+        scatter_vector(FIRST, 0, LENT)
+        scatter_scalar(FIRST, LENT, S)
+        scatter_vector(SECOND, 0, S)
         for b in (FIRST, SECOND):
             nc.sync.dma_start(out=out[b * P : (b + 1) * P, :], in_=window[b][:])

@@ -23,7 +23,7 @@ HALF = S // 2
 QUARTER = S // 4
 LIST_ROWS = 16
 FIRST, SECOND = 0, 1
-LENT = 192
+LENT = 224
 
 
 def tile_picked_kvput_tanh_e_kernel(tc, xT, mem, w1, offs, slot, out):
@@ -166,15 +166,15 @@ def tile_picked_kvput_tanh_e_kernel(tc, xT, mem, w1, offs, slot, out):
         gather_shared(2, HALF)
         gather_shared(3, HALF)
         x_codes[1, 0] = (sb.tile([P, HALF], U32, align_bytes=64, name="x_codes10", tag="x_raw13"), 0)
-        x_codes[1, 1] = (sb.tile([P, HALF], U32, align_bytes=64, name="x_codes11"), HALF)
+        x_codes[1, 1] = (sb.tile([P, HALF], U32, align_bytes=64, name="x_codes11", tag="w_raw1%d" % FIRST), HALF)
         quantize_x(1, 0, HALF)
-        quantize_x(1, HALF, S)
         for b in range(BLOCKS):
             group_w(0, b, nc.scalar.copy)
-        quantize_w(0, FIRST)
         group_w(1, FIRST, nc.vector.tensor_copy)
-        quantize_w(0, SECOND)
+        quantize_w(0, FIRST)
         quantize_w(1, FIRST)
+        quantize_x(1, HALF, S)
+        quantize_w(0, SECOND)
         group_w(1, SECOND, nc.scalar.copy)
         quantize_w(1, SECOND)
         y = {

@@ -191,5 +191,5 @@ def tile_picked_kvput_tanh_e_kernel(tc, xT, mem, w1, offs, slot, out):
         scatter_vector(FIRST, 0, LENT)
         scatter_scalar(FIRST, LENT, S)
         scatter_vector(SECOND, 0, S)
-        for b in (FIRST, SECOND):
-            nc.sync.dma_start(out=out[b * P : (b + 1) * P, :], in_=window[b][:])
+        for b, queue in ((FIRST, nc.scalar), (SECOND, nc.sync)):
+            queue.dma_start(out=out[b * P : (b + 1) * P, :], in_=window[b][:])

@@ -37,6 +37,7 @@ def tile_picked_kvput_tanh_e_kernel(tc, xT, mem, w1, offs, slot, out):
         slot_sb = lists.tile([P, S // LIST_ROWS], U16, name="slot_sb")
         x_rows = xT.rearrange("(g p j) t -> g p j t", g=PASSES, j=PACK)
         w_rows = w1.rearrange("(g p j) c -> g p j c", g=PASSES, j=PACK)
+        w_runs = w1.rearrange("(g p j) c -> g p (j c)", g=PASSES, j=PACK)
         x_raw = {}
         w_raw = {}
         window = {}
@@ -61,11 +62,8 @@ def tile_picked_kvput_tanh_e_kernel(tc, xT, mem, w1, offs, slot, out):
             nc.sync.dma_start(out=raw[:], in_=w_rows[g][:, :, b * P : (b + 1) * P])
             w_raw[g, b] = raw[:]
 
-        def load_w_pass(g):
-            raw = sb.tile([P, PACK, N], F32, align_bytes=64, name="w_raw%d" % g)
-            nc.sync.dma_start(out=raw[:], in_=w_rows[g])
-            for b in range(BLOCKS):
-                w_raw[g, b] = raw[:, :, b * P : (b + 1) * P]
+        def load_w_run(raw, g, e0, e1):
+            nc.sync.dma_start(out=raw[:].rearrange("p j c -> p (j c)")[:, e0:e1], in_=w_runs[g][:, e0:e1])
 
         def group_w(g, b, copy):
             copy(
@@ -131,8 +129,12 @@ def tile_picked_kvput_tanh_e_kernel(tc, xT, mem, w1, offs, slot, out):
         load_x(1, 0, 2)
         load_x(1, 2, 3)
         load_x(1, 3, 4)
-        load_w_pass(0)
+        w_raw0 = sb.tile([P, PACK, N], F32, align_bytes=64, name="w_raw0")
+        for b in range(BLOCKS):
+            w_raw[0, b] = w_raw0[:, :, b * P : (b + 1) * P]
+        load_w_run(w_raw0, 0, 0, PACK * N - P)
         load_w(1, FIRST)
+        load_w_run(w_raw0, 0, PACK * N - P, PACK * N)
         load_w(1, SECOND)
         nc.sync.dma_start(slot_sb[:], slot)
         load_mem(FIRST)
@@ -164,7 +166,13 @@ def tile_picked_kvput_tanh_e_kernel(tc, xT, mem, w1, offs, slot, out):
         nc.vector.tensor_copy(out=picked[1][:, 0:HALF, 1], in_=row1[:])
         nc.vector.tensor_copy(out=picked[1][:, HALF:S, 0:2], in_=pair1[:].rearrange("p t s -> p s t"))
         gather_shared(2, HALF)
-        gather_shared(3, HALF)
+        gather(1, 3, 0, HALF)
+        plain3 = sb.tile([P, HALF], BF16, name="plain3")
+        cuts = range(HALF, S, QUARTER)
+        for s0 in cuts:
+            gather_plain(plain3[:, s0 - HALF : s0 - QUARTER], 1, 3, s0, s0 + QUARTER)
+        for s0 in cuts:
+            nc.vector.tensor_copy(out=picked[1][:, s0 : s0 + QUARTER, 3], in_=plain3[:, s0 - HALF : s0 - QUARTER])
         x_codes[1, 0] = (sb.tile([P, HALF], U32, align_bytes=64, name="x_codes10", tag="x_raw13"), 0)
         x_codes[1, 1] = (sb.tile([P, HALF], U32, align_bytes=64, name="x_codes11", tag="w_raw1%d" % FIRST), HALF)
         quantize_x(1, 0, HALF)

from contextlib import ExitStack

import concourse.mybir as mybir

K, T, S, N, U = 1024, 2048, 512, 256, 1024
FLOPS = 2 * K * S * N

F32 = mybir.dt.float32
BF16 = mybir.dt.bfloat16
U32 = mybir.dt.uint32
U16 = mybir.dt.uint16
U8 = mybir.dt.uint8
FP8X4 = mybir.dt.float8_e4m3fn_x4
TANH = mybir.ActivationFunctionType.Tanh
COPY = mybir.ActivationFunctionType.Copy

P = 128
PACK = 4
K_PASS = P * PACK
PASSES = K // K_PASS
BLOCKS = N // P
HALF = S // 2
QUARTER = S // 4
LIST_ROWS = 16
FIRST, SECOND = 0, 1
LENT = 224


def tile_picked_kvput_tanh_e_kernel(tc, xT, mem, w1, offs, slot, out):
    nc = tc.nc
    with ExitStack() as ctx:
        lists = ctx.enter_context(tc.tile_pool(name="lists", bufs=1))
        sb = ctx.enter_context(tc.tile_pool(name="sb", bufs=1))
        psum = ctx.enter_context(tc.psum_pool(name="psum", bufs=1))

        offs_sb = lists.tile([P, S // LIST_ROWS], U16, name="offs_sb")
        slot_sb = lists.tile([P, S // LIST_ROWS], U16, name="slot_sb")
        x_rows = xT.rearrange("(g p j) t -> g p j t", g=PASSES, j=PACK)
        w_rows = w1.rearrange("(g p j) c -> g p j c", g=PASSES, j=PACK)
        w_runs = w1.rearrange("(g p j) c -> g p (j c)", g=PASSES, j=PACK)
        x_raw = {}
        w_raw = {}
        window = {}

        warm = sb.tile([P, 1], F32, name="warm")
        warm_out = sb.tile([P, 1], F32, name="warm_out")
        nc.vector.memset(warm[:], 0.0)
        nc.scalar.activation(warm_out[:], warm[:], TANH)

        def load_x(g, j0, j1):
            raw = sb.tile([P, j1 - j0, T], F32, align_bytes=64, name="x_raw%d%d" % (g, j0))
            nc.sync.dma_start(out=raw[:], in_=x_rows[g][:, j0:j1, :])
            for j in range(j0, j1):
                x_raw[g, j] = raw[:, j - j0, :]

        def load_mem(b):
            window[b] = sb.tile([P, U], F32, name="window%d" % b)
            nc.sync.dma_start(out=window[b][:], in_=mem[b * P : (b + 1) * P, :])

        def load_w(g, b):
            raw = sb.tile([P, PACK, P], F32, align_bytes=64, name="w_raw%d%d" % (g, b))
            nc.sync.dma_start(out=raw[:], in_=w_rows[g][:, :, b * P : (b + 1) * P])
            w_raw[g, b] = raw[:]

        def load_w_run(raw, g, e0, e1):
            nc.sync.dma_start(out=raw[:].rearrange("p j c -> p (j c)")[:, e0:e1], in_=w_runs[g][:, e0:e1])

        def group_w(g, b, copy):
            copy(
                out=w_grouped[g, b][:].rearrange("p (c i) t -> p c t i", i=4),
                in_=w_raw[g, b].rearrange("p t (c i) -> p c t i", i=4),
            )

        def quantize_w(g, b):
            nc.vector.quantize_mx(
                out=w_codes[g, b][:].bitcast(FP8X4),
                scales=w_scales[g, b][:],
                in_=w_grouped[g, b][:].rearrange("p c t -> p (c t)"),
            )

        def entries(list_sb, s0, s1):
            return list_sb[:, s0 // LIST_ROWS : s1 // LIST_ROWS]

        def gather(g, j, s0, s1):
            nc.vector.tensor_copy(out=picked[g][:, s0:s1, j], in_=x_raw[g, j].indirect(entries(offs_sb, s0, s1)))

        def gather_plain(plain, g, j, s0, s1):
            nc.scalar.activation(plain, x_raw[g, j].indirect(entries(offs_sb, s0, s1)), COPY)

        def gather_shared(j, s0):
            plain = sb.tile([P, S - s0], BF16, name="plain%d" % j)
            gather(1, j, 0, s0)
            gather_plain(plain[:], 1, j, s0, S)
            nc.vector.tensor_copy(out=picked[1][:, s0:S, j], in_=plain[:])

        def codes(g, s0, s1):
            tile, base = x_codes[g, s0 // HALF]
            return tile[:, s0 - base : s1 - base]

        def matmul(g, b, s0, s1):
            nc.tensor.matmul_mx(
                out=acc[b, s0][:],
                lhsT=w_codes[g, b][:].bitcast(FP8X4),
                lhsT_scale=w_scales[g, b][:],
                rhs=codes(g, s0, s1).bitcast(FP8X4),
                rhs_scale=x_scales[g][:, s0:s1],
                start=(g == 0),
                stop=(g == PASSES - 1),
            )

        def quantize_x(g, s0, s1):
            nc.vector.quantize_mx(
                out=codes(g, s0, s1).bitcast(FP8X4),
                scales=x_scales[g][:, s0:s1],
                in_=picked[g][:, s0:s1, :].rearrange("p s t -> p (s t)"),
            )

        def tanh(b, s0, s1, base):
            nc.scalar.activation(y[b][:, s0:s1], acc[b, base][:, s0 - base : s1 - base], TANH)

        def scatter_vector(b, s0, s1):
            nc.vector.tensor_copy(out=window[b][:].indirect(entries(slot_sb, s0, s1)), in_=y[b][:, s0:s1])

        def scatter_scalar(b, s0, s1):
            nc.scalar.activation(window[b][:].indirect(entries(slot_sb, s0, s1)), y[b][:, s0:s1], COPY)

        load_x(0, 0, PACK)
        nc.sync.dma_start(offs_sb[:], offs)
        load_x(1, 0, 2)
        load_x(1, 2, 3)
        load_x(1, 3, 4)
        w_raw0 = sb.tile([P, PACK, N], F32, align_bytes=64, name="w_raw0")
        for b in range(BLOCKS):
            w_raw[0, b] = w_raw0[:, :, b * P : (b + 1) * P]
        load_w_run(w_raw0, 0, 0, PACK * N - P)
        load_w(1, FIRST)
        load_w_run(w_raw0, 0, PACK * N - P, PACK * N)
        load_w(1, SECOND)
        nc.sync.dma_start(slot_sb[:], slot)
        load_mem(FIRST)
        load_mem(SECOND)

        first_pieces = [(FIRST, 0, QUARTER), (FIRST, QUARTER, HALF), (FIRST, HALF, S)]
        second_pieces = [(SECOND, 0, HALF), (SECOND, HALF, S)]
        acc = {(b, s0): psum.tile([P, s1 - s0], F32, name="acc%d_%d" % (b, s0)) for b, s0, s1 in first_pieces[:2] + second_pieces}
        picked = [sb.tile([P, S, PACK], BF16, align_bytes=64, name="picked%d" % g) for g in range(PASSES)]
        codes0 = sb.tile([P, S], U32, align_bytes=64, name="x_codes0")
        x_codes = {(0, h): (codes0, 0) for h in range(2)}
        x_scales = [sb.tile([P, S], U8, align_bytes=64, name="x_scales%d" % g) for g in range(PASSES)]
        both = [(g, b) for g in range(PASSES) for b in range(BLOCKS)]
        w_codes = {gb: sb.tile([P, P], U32, align_bytes=64, name="w_codes%d%d" % gb) for gb in both}
        w_scales = {gb: sb.tile([P, P], U8, align_bytes=64, name="w_scales%d%d" % gb) for gb in both}
        w_grouped = {gb: sb.tile([P, P, PACK], BF16, align_bytes=64, name="w_grouped%d%d" % gb) for gb in both}
        pair = sb.tile([P, 2, S], F32, name="pair")
        for j in range(2):
            gather(0, j, 0, S)
            gather_plain(pair[:, j, :], 0, 2 + j, 0, S)
        nc.vector.tensor_copy(out=picked[0][:, :, 2:PACK], in_=pair[:].rearrange("p t s -> p s t"))
        quantize_x(0, 0, S)
        row1 = sb.tile([P, HALF], F32, name="row1")
        pair1 = sb.tile([P, 2, HALF], F32, name="pair1")
        gather(1, 0, 0, HALF)
        gather_plain(row1[:], 1, 1, 0, HALF)
        for j in range(2):
            gather_plain(pair1[:, j, :], 1, j, HALF, S)
        nc.vector.tensor_copy(out=picked[1][:, 0:HALF, 1], in_=row1[:])
        nc.vector.tensor_copy(out=picked[1][:, HALF:S, 0:2], in_=pair1[:].rearrange("p t s -> p s t"))
        gather_shared(2, HALF)
        gather(1, 3, 0, HALF)
        plain3 = sb.tile([P, HALF], BF16, name="plain3")
        cuts = range(HALF, S, QUARTER)
        for s0 in cuts:
            gather_plain(plain3[:, s0 - HALF : s0 - QUARTER], 1, 3, s0, s0 + QUARTER)
        for s0 in cuts:
            nc.vector.tensor_copy(out=picked[1][:, s0 : s0 + QUARTER, 3], in_=plain3[:, s0 - HALF : s0 - QUARTER])
        x_codes[1, 0] = (sb.tile([P, HALF], U32, align_bytes=64, name="x_codes10", tag="x_raw13"), 0)
        x_codes[1, 1] = (sb.tile([P, HALF], U32, align_bytes=64, name="x_codes11", tag="w_raw1%d" % FIRST), HALF)
        quantize_x(1, 0, HALF)
        for b in range(BLOCKS):
            group_w(0, b, nc.scalar.copy)
        group_w(1, FIRST, nc.vector.tensor_copy)
        quantize_w(0, FIRST)
        quantize_w(1, FIRST)
        quantize_x(1, HALF, S)
        quantize_w(0, SECOND)
        group_w(1, SECOND, nc.scalar.copy)
        quantize_w(1, SECOND)
        y = {
            FIRST: sb.tile([P, S], F32, align_bytes=64, name="y_first", tag="w_raw1%d" % SECOND),
            SECOND: sb.tile([P, S], F32, name="y_second"),
        }
        pieces = first_pieces[:2] + second_pieces + first_pieces[2:]
        for b, s0, s1 in pieces:
            if (b, s0) not in acc:
                acc[b, s0] = psum.tile([P, s1 - s0], F32, name="acc_last", tag="acc%d_%d" % (FIRST, QUARTER))
            for g in range(PASSES):
                matmul(g, b, s0, s1)
            tanh(b, s0, s1, s0)
        scatter_vector(FIRST, 0, LENT)
        scatter_scalar(FIRST, LENT, S)
        scatter_vector(SECOND, 0, S)
        for b, queue in ((FIRST, nc.scalar), (SECOND, nc.sync)):
            queue.dma_start(out=out[b * P : (b + 1) * P, :], in_=window[b][:])
